import numpy as np, ml_dtypes
CORES = [36,164,52,180,100,228,116,244]
N = 8
BF = ml_dtypes.bfloat16
def gentries(a):
    return np.ascontiguousarray(a.reshape(8, 16, -1).transpose(0, 2, 1)).reshape(8, -1)
def gtable(e):
    e = np.asarray(e); return np.ascontiguousarray(e.reshape(8, -1, 16).transpose(0, 2, 1)).reshape(128, -1).astype(np.int32)
M, D, SD, Q, SQ, L, V = 144, 16, 8, 4, 10, 128, 4
W, P = M * D, M * Q
def unpack(x):
    x = np.ascontiguousarray(x.astype(np.int64).reshape(N, 8, 16, -1).transpose(0, 1, 3, 2)); return x >> 8, x & 255
def pick(x, i):
    return np.take_along_axis(x, i[..., None], 2)
def cut(lb, lm, pb, pm):
    o = np.argsort(np.concatenate([2 * lb, 2 * pb + 1], axis=-1), axis=-1, kind="stable")
    z = np.take_along_axis(np.concatenate([lb, pb], axis=-1), o, -1); lane = (o < 16).astype(np.int64)
    na = np.add.accumulate(lane, axis=-1) - 1; nb = np.maximum(np.add.accumulate(1 - lane, axis=-1) - 1, 0)
    ln = np.concatenate([z[..., 1:], np.full(z.shape[:-1] + (1,), 4096)], axis=-1) - z
    return z, ln, np.take_along_axis(lm, na, -1), np.take_along_axis(pm, nb, -1)
def weigh(tot, z, ln, a, b):
    ia = D * a + (z >> SD); ib = D * b + (z >> SD)
    sa = np.take_along_axis(tot, ia.reshape(N, 8, -1), 2).reshape(z.shape); sb = np.take_along_axis(tot, ib.reshape(N, 8, -1), 2).reshape(z.shape)
    w = ln * (sa + sb)
    return ia, ib, np.where(sb > sa, b, a), w, np.add.accumulate(w, axis=-1)
def remake(z, ln, den, vis, pb, pm):
    live = vis & (ln > 0)
    last = np.maximum.accumulate(np.where(live, np.arange(32), -1), axis=-1); e = last[..., -1:]
    zz = np.take_along_axis(z, e, -1); name = (Q * np.take_along_axis(den, e, -1) + (zz >> SQ))[..., 0]
    before = np.concatenate([np.full_like(e, -1), last[..., :-1]], axis=-1)
    new = live & ((before < 0) | (den != np.take_along_axis(den, np.maximum(before, 0), -1)))
    place = np.add.accumulate(new.astype(np.int64), axis=-1) - 1
    tb, tm = pick(pb, name), pick(pm, name); late = tb > zz
    tp = place[..., -1:] + np.add.accumulate(late.astype(np.int64), axis=-1)
    to = np.minimum(np.concatenate([np.where(new, place, 16), np.where(late, tp, 16)], axis=-1), 16)
    fb = np.full(z.shape[:-1] + (17,), 4095, np.int64); fm = np.zeros(fb.shape, np.int64)
    np.put_along_axis(fb, to, np.concatenate([z, tb], axis=-1), -1); np.put_along_axis(fm, to, np.concatenate([den, tm], axis=-1), -1)
    return fb[..., :16], fm[..., :16], name
def hand(fb, fm, name):
    return np.roll(fb, 1, axis=0), np.roll(fm, 1, axis=0), np.roll(name, (1, 1), axis=(0, 1))
def begins(rng, *shape):
    b = np.sort((4096 * rng.random(shape + (16,)) ** rng.choice(np.array([1, 1, 2, 3]), shape + (1,))).astype(np.int64), axis=-1); b[..., 0] = 0
    again = rng.random(b.shape) < 0.06; again[..., 0] = False
    b = np.where(again, np.concatenate([b[..., :1], b[..., :-1]], axis=-1), b)
    return np.where(rng.random(shape + (1,)) < 0.3, b & ~31, b)
def media(rng, *shape):
    m = rng.integers(0, M, shape + (16,)); same = rng.random(m.shape) < 0.15; same[..., 0] = False
    return np.where(same, np.concatenate([m[..., :1], m[..., :-1]], axis=-1), m)
def level(rng, t):
    return (t + (np.arange(16)[:, None] + rng.integers(0, 16, (N, 8, 1, W))) % 16) // 16
def paint(rng, share, own):
    return np.exp2(2 * (share * rng.random(own) + (1 - share) * rng.random((N, 8, 16, W))) - 1)
def parts(rng):
    lb, lm, pb, pm = begins(rng, N, 8, L), media(rng, N, 8, L), begins(rng, N, 8, P), media(rng, N, 8, P)
    sg = (rng.random((N, 8, 16, W)) * (rng.integers(1, 16, (N, 8, 1, W)) + 1)).astype(np.int64)
    co = paint(rng, 0.5, (N, 8, 16, 1)).reshape(N, 128, W).astype(np.float32).astype(BF)
    u = rng.random((N, 8, V, L)); om = np.where(rng.random(u.shape) < 0.5, np.exp2(12 + 9 * u), 1 + 2 ** 20 * u).astype(np.int64)
    return lb, lm, pb, pm, rng.integers(0, P, (N, 8, L)), sg, co, np.minimum(om, 2 ** 21)
def pack(lb, lm, pb, pm, fp, sg, co, om):
    ls, px = [np.ascontiguousarray((256 * b + m).transpose(0, 1, 3, 2).reshape(N, 128, -1)).astype(np.int32) for b, m in ((lb, lm), (pb, pm))]
    return {"sg": np.ascontiguousarray(sg.reshape(N, 128, W)).astype(np.float32).astype(BF), "co": co, "px": px, "ls": ls,
            "fp": np.stack([gtable(a) for a in fp]), "om": np.stack([gtable(a.reshape(8, -1)) for a in om])}
def plant(lb, lm, pb, pm, pn, sg, choose):
    tot = np.add.reduce(sg, axis=2); om = []
    for v in range(V):
        z, ln, a, b = cut(lb, lm, pick(pb, pn), pick(pm, pn)); ia, ib, den, w, cum = weigh(tot, z, ln, a, b)
        t = np.clip(choose(ln, w, cum), 1, 2 ** 21); om.append(t)
        lb, lm, pn = hand(*remake(z, ln, den, cum - w < t[..., None], pb, pm))
    return np.stack(om, axis=2)
def setup_inputs(rng):
    return pack(*parts(rng))
def setup_inputs_spread(rng):
    lb, lm, pb, pm, fp, sg, co, om = parts(rng)
    hi = np.minimum(np.exp2(2.1 + 2.1 * rng.random((N, 8, 1, W))).astype(np.int64) - 1, 15)
    sg = (rng.random((N, 8, 16, W)) * (hi + 1)).astype(np.int64) * (rng.random((N, 8, 1, W)) > 0.0625)
    co = paint(rng, 0.8, (N, 8, 1, W)).reshape(N, 128, W).astype(np.float32).astype(BF)
    u = rng.random((N, 8, V, L)); om = np.minimum(np.where(rng.random(u.shape) < 0.5, np.exp2(21 * u), 1 + 2 ** 21 * u).astype(np.int64), 2 ** 21)
    return pack(lb, lm, pb, pm, fp, sg, co, om)
def setup_inputs_ends(rng):
    lb, lm, pb, pm, fp, sg, co, om = parts(rng); i = np.arange(16)
    t = ((N - 1 - np.arange(N)[:, None] + 7 - np.arange(8)[None, :]) % 4)[:, :, None, None]
    sg = 15 * np.where(t == 0, 1, np.where(t == 1, rng.integers(0, 2, (N, 8, 1, W)), np.where(t == 2, rng.integers(0, 2, (N, 8, 16, W)), 0)))
    def some(n):
        first = i < rng.integers(1, 16, (N, 8, n, 1)); u = rng.random((N, 8, n, 1))
        b = np.where(u < 0.83, np.where(first, 0, 4095), begins(rng, N, 8, n))
        m = np.where(u < 0.66, np.where(first, 0, M - 1), np.where(u < 0.83, np.where(first, M - 1, 0), (M - 1) * rng.integers(0, 2, (N, 8, n, 16))))
        return b, m
    lb, lm = some(L); pb, pm = some(P); b0 = np.where(i < 15, 0, 4095); m0 = np.where(i < 15, 0, M - 1)
    lb[:, :, [0, 1, L - 2, L - 1]] = b0; lm[:, :, [0, 1, L - 2, L - 1]] = m0; pb[:, :, [0, P - 1]] = b0; pm[:, :, [0, P - 1]] = m0
    pb[:, :, [1, 2, P - 3, P - 2]] = begins(rng, N, 8, 4); pm[:, :, [1, 2, P - 3, P - 2]] = (M - 1) * rng.integers(0, 2, (N, 8, 4, 16))
    fp = (P - 1) * rng.integers(0, 2, (N, 8, L))
    whole = [2, 3, L - 4, L - 3]; pb[:, :, P - 1] = 0
    lb[:, :, whole] = 0; lm[:, :, whole] = m0; fp[:, :, whole] = P - 1
    om = np.where(rng.random(om.shape) < 0.7, np.where(rng.random(om.shape) < 0.4, 1, 2 ** 21), rng.choice(np.array([479, 480, 481, 480 * 4095, 480 * 4095 + 1, 480 * 4096 - 1, 480 * 4096, 480 * 4096 + 1]), om.shape))
    om[..., [0, L - 1]] = 480 * 4095 + 1; om[..., [1, L - 2]] = 480 * 4095
    om[:, :, 0, 2] = 480 * 4096; om[:, :, 0, L - 3] = 480 * 4096; om[:, :, 0, 3] = 2 ** 21; om[:, :, 0, L - 4] = 2 ** 21
    return pack(lb, lm, pb, pm, fp, sg, co, om)
def setup_inputs_corners(rng):
    lb, lm, pb, pm, fp, sg, co, om = parts(rng); i = np.arange(16)
    kind = (np.arange(N)[:, None] + np.arange(8)[None, :]) % 4; k4 = kind[:, :, None, None]
    sg = np.where(k4 == 0, level(rng, np.arange(W) // D * 240 // (M - 1)), np.where(k4 == 2, level(rng, rng.integers(1, 240, (N, 8, 1, 1))), sg))
    runs = rng.choice(np.array([1, 2, 3, 15, 16, 16, 17, 31]), (N, 8, L, 1)); own = rng.integers(np.maximum(1, runs - 15), np.minimum(16, runs) + 1)
    steps = 120 * i + rng.integers(0, 100, (N, 8, L, 16)); steps[..., 0] = 0
    lb = np.where(k4 == 0, steps, lb); lm = np.where(k4 == 0, rng.integers(2, M // 4, (N, 8, L, 1)) + 4 * (np.minimum(i, own - 1) % 2), lm)
    kk = np.arange(16)[:, None]; late = i >= 16 - kk
    pb[:, :, P - 16:] = np.where(k4 == 0, np.where(late, 2100 + 120 * (i - 16 + kk) + rng.integers(0, 100, (N, 8, 16, 16)), 0), pb[:, :, P - 16:])
    pm[:, :, P - 16:] = np.where(k4 == 0, np.where(late, M // 2 + 4 + 4 * (i % 2), 0), pm[:, :, P - 16:])
    one = np.repeat(fp[:, :, :1], L, axis=2); one[:, :, L - 1] = (one[:, :, L - 1] + 1) % P
    fp = np.where(kind[:, :, None] == 0, P - 16 + (runs - own)[..., 0], np.where(kind[:, :, None] == 1, one, fp))
    sel = rng.integers(0, 4, (N, 8, L, 1)); at = np.where(sel == 0, 0, np.where(sel == 1, 4095, rng.integers(1, 4096, (N, 8, L, 1))))
    lb = np.where((k4 == 1) & (sel < 3), np.where(i == 0, 0, at), lb)
    lb = np.where(k4 == 3, pick(pb, fp), lb)
    om = np.where((k4 == 1) & (rng.random(om.shape) < 0.5), 1, om)
    om[:, :, 0] = np.where((kind[:, :, None] == 0) & (rng.random((N, 8, L)) < 0.75), 2 ** 21, om[:, :, 0])
    return pack(lb, lm, pb, pm, fp, sg, co, om)
def setup_inputs_ties(rng):
    lb, lm, pb, pm, fp, sg, co, om = parts(rng); lb = lb & ~255; pb = np.where(rng.random((N, 8, P, 1)) < 0.8, pb & ~255, pb)
    sg = level(rng, rng.choice(np.array([40, 41, 120, 239, 240]), (N, 8, 1, W)))
    def choose(ln, w, cum):
        e = rng.integers(0, 32, (N, 8, L, 1)); return (np.take_along_axis(cum, e, -1) + rng.integers(0, 2, e.shape))[..., 0]
    return pack(lb, lm, pb, pm, fp, sg, co, plant(lb, lm, pb, pm, fp, sg, choose))
def setup_inputs_calm(rng):
    lb, lm, pb, pm, fp, sg, co, om = parts(rng); low = np.where(np.arange(8) % 2 == 0, 0, M - 2)[None, :, None, None]
    sg = rng.integers(4, 16, (N, 8, 16, W))
    def near(n):
        u = rng.integers(0, 3, (N, 8, n, 1)); x = np.sort(rng.integers(0, 26, (N, 8, n, 16)), axis=-1)
        b = np.where(u == 0, x, np.where(u == 1, 4070 + x, begins(rng, N, 8, n))); b[..., 0] = 0
        return b, low + rng.integers(0, 2, (N, 8, n, 16))
    lb, lm = near(L); pb, pm = near(P); fp = rng.choice(np.array([0, 1, 2, 3, P - 2, P - 1]), (N, 8, L))
    def choose(ln, w, cum):
        o = np.argsort(ln == 0, axis=-1, kind="stable"); n = np.add.reduce((ln > 0).astype(np.int64), axis=-1, keepdims=True)
        k = rng.integers(0, 6, n.shape); k = np.maximum(np.where(k < 4, np.minimum(k, n - 1), n - 1 - (k - 4)), 0)
        e = np.take_along_axis(o, k, -1); hit = np.take_along_axis(cum, e, -1)
        return np.where(rng.random(n.shape) < 0.5, hit, hit - np.take_along_axis(w, e, -1) + 1)[..., 0]
    return pack(lb, lm, pb, pm, fp, sg, co, plant(lb, lm, pb, pm, fp, sg, choose))
def check_ranges(d):
    bad = []; s = d["sg"].astype(np.float32); c = d["co"].astype(np.float32)
    if not np.all((s >= 0) & (s <= 15) & (s == np.floor(s))): bad.append("range of sg")
    if not np.all((c >= 0.5) & (c <= 2)): bad.append("range of co")
    for k, lo, hi in (("px", 0, 4095 * 256 + M - 1), ("ls", 0, 4095 * 256 + M - 1), ("fp", 0, P - 1), ("om", 1, 2 ** 21)):
        if np.min(d[k]) < lo or np.max(d[k]) > hi: bad.append("range of " + k)
    for k in ("px", "ls"):
        b, m = unpack(d[k])
        if np.max(m) >= M: bad.append("media of " + k)
        if np.any(b[..., 0] != 0) or np.any(b[..., 1:] < b[..., :-1]): bad.append("begins of " + k)
    return bad
def reference(sg, co, px, ls, fp, om):
    s = sg.astype(np.float64).reshape(N, 8, 16, W); c = co.astype(np.float64).reshape(N, 8, 16, W); tot = np.add.reduce(s, axis=2).astype(np.int64)
    pb, pm = unpack(px); lb, lm = unpack(ls); pn = np.stack([gentries(a) for a in fp]).astype(np.int64)
    bound = np.stack([gentries(a) for a in om]).astype(np.int64).reshape(N, 8, V, L)
    yc = np.zeros((N, 8, 16, V, L), np.float32); yt = np.zeros((N, 8, 16, V, L), np.float32)
    for v in range(V):
        z, ln, a, b = cut(lb, lm, pick(pb, pn), pick(pm, pn)); ia, ib, den, w, cum = weigh(tot, z, ln, a, b)
        vis = cum - w < bound[:, :, v, :, None]; seen = np.where(vis, ln, 0)
        for q in range(N):
            for g in range(8):
                ja, jb = ia[q, g].reshape(-1), ib[q, g].reshape(-1)
                tau = ((np.take(s[q, g], ja, 1) + np.take(s[q, g], jb, 1)) * seen[q, g].reshape(-1) * 2.0 ** -14).reshape(16, L, 32)
                al = tau * 0.125; tr = np.ones_like(al); tr[..., 1:] = np.multiply.accumulate(1.0 - al, axis=-1)[..., :-1]
                cc = (np.take(c[q, g], ja, 1) + np.take(c[q, g], jb, 1)).reshape(16, L, 32)
                yc[q, g, :, v] = np.add.reduce(tr * al * cc, axis=-1); yt[q, g, :, v] = np.add.reduce(tau, axis=-1)
        if v < V - 1: lb, lm, pn = hand(*remake(z, ln, den, vis, pb, pm))
    return {"yc": yc.reshape(N, 128, V * L), "yt": yt.reshape(N, 128, V * L)}

def check_inputs(d):
    bad = list(check_ranges(d))
    if not bad:
        for name, y in reference(**d).items():
            for q in range(N):
                v = np.abs(np.asarray(y[q], np.float64)); s = np.sqrt(np.mean(v * v))
                if v.max() > 7 * s or s < 2.0 ** -3: bad.append('%s of rank %d is uneven or too small' % (name, q))
    return bad

@@ -1,0 +1,644 @@
+import numpy as np
+from concourse.mybir import AluOpType, ActivationFunctionType
+
+F, B, I, U = "float32", "bfloat16", "int32", "uint16"
+NV = 4
+WT = 2320
+SCRATCH = {}
+
+
+def _s(names, n, d):
+    for x in names.split():
+        SCRATCH[x] = ("sbuf", [128, n], d)
+
+
+_s("tsg tco", WT, B)
+_s("pxi pxh", 576, I); _s("pk", 576, F); _s("lsi", 128, I)
+_s("fpi", 8, I); _s("omi", 32, I); _s("omf nb", 32, F); _s("omx", 512, F)
+_s("sel", 2048, B)
+_s("ones id32 id16 ppx pls ptl posc idp idn", 128, F); _s("idb nidb idc", 128, B)
+_s("dgi", 144, I); _s("dg", 144, F); _s("blk", 8, F); _s("rh", 48, B)
+_s("pid", 8, I); _s("col", 16, F); _s("oci", 64, I); _s("oc", 64, U)
+_s("rst0 rstm rstb sc cz", 256, F); _s("oneb", 512, B)
+_s("l0 l1 l2 l3 o0 o1 o2", 128, F); _s("n0 n1 n2 n3 m0 m1 m2 nown", 8, U)
+_s("pe te ma mb", 128, F); _s("mm", 256, F)
+_s("ki xi zs ei e1 e2 e3", 256, I)
+_s("xf yf af bf ln zc nw lv den xa xb zz nm tc vh", 256, F); _s("ff", 264, F); _s("slb", 256, B)
+_s("oa0 oa1 ob0 ob1", 256, U); _s("lh0 lh1", 512, B)
+_s("t8 n8 nam thr", 8, F); _s("q8", 8, I); _s("nx", 144, F)
+_s("thb tm ta tb nk nu nw1 nz nkk uu", 128, F); _s("nzi", 128, I)
+_s("sa0 sa1 sb0 sb1", 4096, B); _s("ca0 ca1 cb0 cb1", 4112, B)
+_s("al0 al1 ub om0 om1", 4096, F); _s("yo0 yo1", 256, F)
+for _k in range(8):
+    SCRATCH["p%d" % _k] = ("psum", [128, 512], F)
+NDS = 48
+SEMAPHORES = ["sv", "ss", "sp", "sgq"] + ["d%d" % k for k in range(NDS)] + ["rn0", "rn1", "rn2", "rl0", "rl1", "rl2"]
+
+A = AluOpType
+ACT = ActivationFunctionType
+M1, M2 = 33825.0, 585.0
+TWO24 = 16777216.0
+KF = 2047 * 8192.0 + 3840.0
+
+CY, PCY, GA, LAT = 1.0, 0.5, 1.56, 90.0
+DL, DR, RL, RR = 1800.0, 200.0, 1500.0, 60.0
+SG = ['vvsvsssv', 'sssvvsvs', 'svvssvss', 'svsvsvsv']
+CO = ['sssvsssv', 'ssssssss', 'ssssssss', 'sssvssvs']
+OM = ['ssvsssvs', 'ssssssvv', 'ssssssss', 'svsssvss']
+SIDE = 'sssssssv'
+FOLD = ['dd', 'pd', 'dd', 'dd']
+AH = [2, 2, 2, 1]
+CQ = 4
+OLN = 1
+BANKA = ['15151515', '15151515', '15615615', '14321432']
+BANKS = ['56156156', '65165165', '65165165', '56143256']
+URG = {'c': [52, 0, -8, -68], 'a': [68, 34, 30, -172], 'o': [49, 10, 15, -84], 'u': [60, 34, 4, -80], 'y': [34, 30, -41, -64]}
+HOLD = {'v': 0.3, 's': 0.7, 'p': 0.8, 'g': 1.0, 'y': 0.0}
+LOOK = 0.2
+PLAN = {}
+
+
+def rank_program(g, core, T, topo):
+    rank = T.rank_of(core)
+    if rank is None:
+        return
+    nxt = T.cores[(rank + 1) % len(T.cores)]
+    rid, pid = topo.addr(nxt, core)
+    mask = topo.mask(core, nxt)
+    neng = len(topo.engines(core, nxt))
+    Q = {"v": g.vector, "s": g.scalar, "p": g.tensor, "g": g, "y": g.sync}
+    ops = []
+    wr, rd, ep = {}, {}, {}
+    nd = [0]
+    tag = ["k"]
+
+    def R(name, a=0, b=None, st=1):
+        if b is None:
+            b = SCRATCH[name][1][1]
+        if st > 0:
+            return (T[name][:, a:b:st] if st > 1 else T[name][:, a:b], name, np.arange(a, b, st))
+        return (T[name][:, b - 1:(a - 1 if a > 0 else None):-1], name, np.arange(a, b))
+
+    def G(win, off):
+        return (win[0].indirect(off[0]), win[1], win[2], off)
+
+    def add(eng, fn, reads, writes, cost, lat=0.0, sem=None):
+        me = len(ops); deps = set(); order = set()
+        rs = []
+        for r in reads:
+            if isinstance(r, tuple):
+                rs.append(r)
+                if len(r) == 4:
+                    rs.append(r[3])
+        for r in rs + writes:
+            nme = r[1]
+            if nme not in wr:
+                wr[nme] = np.full(SCRATCH[nme][1][1], -1); rd[nme] = []
+            if SCRATCH[nme][0] == "psum":
+                e = ep.setdefault(nme, [eng, [], []])
+                if e[0] != eng:
+                    ep[nme] = e = [eng, [], e[1]]
+                deps.update(e[2])
+                if eng == "p":
+                    order.update(e[1])
+                if me not in e[1]:
+                    e[1].append(me)
+        for r in rs:
+            deps.update(int(x) for x in np.unique(wr[r[1]][r[2]]) if x >= 0)
+        for w in writes:
+            for x in np.unique(wr[w[1]][w[2]]):
+                if x >= 0 and not (eng == "p" and ops[int(x)]["e"] == "p"):
+                    deps.add(int(x))
+            m = np.zeros(len(wr[w[1]]), bool); m[w[2]] = True
+            keep = []
+            for o, c in rd[w[1]]:
+                if m[c].any():
+                    deps.add(o)
+                    c = c[~m[c]]
+                if len(c):
+                    keep.append((o, c))
+            rd[w[1]] = keep
+        for r in rs:
+            rd[r[1]].append((me, r[2]))
+        for w in writes:
+            wr[w[1]][w[2]] = me
+        deps.discard(me); order.discard(me)
+        ops.append({"e": eng, "f": fn, "d": deps, "o": order, "c": cost, "l": lat, "sem": sem, "t": tag[0]})
+        return me
+
+    def ap(x):
+        return x[0] if isinstance(x, tuple) else x
+
+    def ps(x):
+        return SCRATCH[x[1]][0] == "psum"
+
+    def vc(o, i, k=1.0):
+        n = len(o[2])
+        return 50 + n * GA * CY if len(i) == 4 else max(64, n * k) * CY
+
+    def tt(o, a, b, op):
+        return add("v", lambda: g.vector.tensor_tensor(o[0], a[0], b[0], op), [a, b], [o], vc(o, a, 1.0 if ps(a) or ps(b) else 2.0))
+
+    def ts(o, a, s1, op0, s2=None, op1=None):
+        if op1 is None:
+            return add("v", lambda: g.vector.tensor_scalar(o[0], a[0], ap(s1), None, op0), [a, s1], [o], vc(o, a))
+        return add("v", lambda: g.vector.tensor_scalar(o[0], a[0], ap(s1), ap(s2), op0, op1), [a, s1, s2], [o], vc(o, a))
+
+    def cp(o, a):
+        return add("v", lambda: g.vector.tensor_copy(o[0], a[0]), [a], [o], vc(o, a))
+
+    def ms(o, c):
+        return add("v", lambda: g.vector.memset(o[0], c), [], [o], max(64, len(o[2])) * CY)
+
+    def scan(o, a, b, init, op0, op1):
+        return add("v", lambda: g.vector.tensor_tensor_scan(o[0], a[0], b[0], init, op0, op1), [a, b], [o], vc(o, a))
+
+    def act(o, a, scale=1.0, bias=0.0, fn=ACT.Copy):
+        if bias == 0.0 and scale == 1.0:
+            return add("s", lambda: g.scalar.activation(o[0], a[0], fn), [a], [o], vc(o, a) + 15)
+        return add("s", lambda: g.scalar.activation(o[0], a[0], fn, bias=bias, scale=scale), [a], [o], vc(o, a) + 15)
+
+    def un(eng, o, a, scale, bias):
+        if eng == "v":
+            ts(o, a, scale, A.mult, bias, A.add)
+        else:
+            act(o, a, scale, bias)
+
+    def gather(eng, o, w):
+        if eng == "v":
+            cp(o, w)
+        else:
+            act(o, w)
+
+    def mm(lst):
+        def fn():
+            r = None
+            for o, l, x, a, b in lst:
+                r = g.tensor.matmul(o[0], l[0], x[0], a, b)
+            return r
+        c = sum(max(64, len(x[2])) * (4 if SCRATCH[x[1]][2] == F else 1) for o, l, x, a, b in lst) * PCY
+        return add("p", fn, [q[1] for q in lst] + [q[2] for q in lst], [q[0] for q in lst], c, 60.0)
+
+    def iota(o, pat, base, cm):
+        if SCRATCH[o[1]][2] == I:
+            fn = lambda: g.iota(o[0], pat, base, cm)
+        else:
+            fn = lambda: g.iota(o[0], pat, base, cm, allow_small_or_imprecise_dtypes=True)
+        return add("g", fn, [], [o], 130 + 2 * len(o[2]) * CY)
+
+    def asel(o, a, pat, base):
+        return add("g", lambda: g.affine_select(o[0], a[0], pat, A.is_equal, 0.0, base, -1), [a], [o], 170 + 2 * len(o[2]) * CY)
+
+    def newsem():
+        nd[0] += 1
+        return "d%d" % (nd[0] - 1)
+
+    def dma(eng, o, i, reads, writes, nbytes, **kw):
+        s = newsem()
+        return add(eng, lambda: Q[eng].dma_start(o, i, **kw).then_inc(T.sem[s], 16), reads, writes,
+                   900.0 if eng == "g" else 60.0, DL + nbytes / DR, (s, 16))
+
+    def send(src, dst, rs, nbytes):
+        s = newsem()
+        a = add("g", lambda: g.remote_dma(dst[0], src[0], T.sem[rs], T.sem[s], pid, rid, mask), [src], [], 300.0, 1000.0, (s, neng))
+        b = add("r", None, [], [dst], 0.0, RL + nbytes / RR, (rs, neng))
+        ops[b]["o"].add(a)
+
+    dma("y", R("lsi")[0], T.ls[:], [], [R("lsi")], 65536)
+    dma("s", R("pxi")[0], T.px[:], [], [R("pxi")], 294912)
+    dma("y", R("fpi")[0], T.fp[:], [], [R("fpi")], 4096)
+    dma("y", R("tsg", 0, 2304)[0], T.sg[:], [], [R("tsg", 0, 2304)], 589824)
+    dma("s", R("omi")[0], T.om[:], [], [R("omi")], 16384)
+    dma("y", R("tco", 0, 2304)[0], T.co[:], [], [R("tco", 0, 2304)], 589824)
+
+    ms(R("ones"), 1.0)
+    iota(R("pid", 0, 1), [[0, 1]], 0, 1)
+    asel(R("pls"), R("ones"), [[16, 4], [1, 16], [64, 2]], 0)
+    asel(R("ppx"), R("ones"), [[16, 4], [-1, 16], [64, 2]], 15)
+    iota(R("xa"), [[0, 4], [1, 2], [0, 32]], 0, 0)
+    asel(R("id32"), R("ones"), [[1, 128]], 0)
+    iota(R("q8"), [[-16, 8]], 0, 1)
+    iota(R("xb"), [[0, 8], [1, 32]], 0, 0)
+    iota(R("dgi"), [[0, 9], [-1, 16]], 16, 1)
+    iota(R("oci", 0, 32), [[1, 32]], 0, 0)
+    iota(R("oci", 32, 42), [[1, 10]], 7, 0)
+    iota(R("oci", 48, 56), [[0, 8]], 0, 1)
+    asel(R("ptl"), R("ones"), [[1, 16], [16, 8]], 0)
+    for q in range(4):
+        iota(R("posc", 32 * q, 32 * q + 32), [[-16384, 2], [-32768, 2], [0, 8]], (16 - (q >> 1) - 2 * (q & 1)) * 4096, 0)
+    act(R("sel"), R("tsg", 0, 2048), 0.0, 1.0)
+    tag[0] = "f0a"
+    asel(R("sel"), R("sel"), [[1, 16], [16, 8], [0, 16]], 0)
+    tag[0] = "k"
+
+    def C(k):
+        return R("col", k, k + 1)
+
+    def P(k):
+        return R("pid", k, k + 1)
+    ts(P(1), P(0), 15, A.bitwise_and)
+    ts(P(2), P(0), 4, A.arith_shift_right, 1, A.bitwise_and)
+    ts(C(0), P(1), 256.0, A.mult, -TWO24, A.add)
+    ts(C(1), P(1), 256.0, A.mult, 4096.0 - TWO24, A.add)
+    ts(C(2), P(1), 0.0, A.is_equal)
+    ts(C(5), C(2), -1048576.0, A.mult, -128.0, A.add)
+    ts(C(6), C(2), -1048576.0, A.mult, -128.0 - 65536.0, A.add)
+    ts(C(7), C(2), 2304.0, A.mult)
+    ts(C(8), C(2), 4096.0, A.mult)
+    ts(C(9), P(2), -2.0, A.mult)
+    ts(C(10), P(2), 2.0, A.mult, -2.0, A.add)
+    act(R("id16"), R("id32"), 16.0); act(R("idb"), R("id32")); act(R("nidb"), R("id32"), -1.0)
+    act(R("idp"), R("id32"), 1.0 / 512); act(R("idn"), R("id32"), -1.0 / 512); act(R("idc"), R("id32"), -8.0)
+    ts(R("q8"), R("q8"), 4, A.arith_shift_right)
+    ts(R("blk"), R("q8"), 0.0, A.is_equal)
+    for k, x in enumerate((-4096.0, -1.0, -4096.0, 1.0, 4096.0, 1.0)):
+        act(R("rh", 8 * k, 8 * k + 8), R("blk"), x)
+    ts(R("dgi"), R("dgi"), 15, A.bitwise_and)
+    ts(R("dg"), R("dgi"), 0.0, A.is_equal)
+    ts(R("oci", 32, 42), R("oci", 32, 42), 7, A.bitwise_and)
+    ts(R("oci", 48, 56), R("oci", 48, 56), 7, A.bitwise_and)
+    cp(R("oc", 0, 42), R("oci", 0, 42)); cp(R("oc", 48, 56), R("oci", 48, 56))
+    act(R("oneb", 256, 512), R("xa"), 1.0 / 512)
+    act(R("cz"), R("xa"), 1.0 / 512, 2047 + 255.0 / 256)
+    act(R("zz"), R("xb"), fn=ACT.Sign)
+    act(R("rstm"), R("zz"), 4194304.0, -M1)
+    act(R("rstb"), R("zz"), -65536.0, 65536.0)
+    act(R("rst0"), R("zz"), 0.0)
+    act(R("sc"), R("xb"), -M1, 32 * M1)
+    act(R("oneb", 0, 256), R("xb"), 0.0, 1.0)
+    ms(R("tsg", 2304, WT), 16.0); ms(R("tco", 2304, WT), 0.0)
+    for x in ("ca0", "ca1", "cb0", "cb1"):
+        ms(R(x, 4096, 4112), 0.0)
+    ms(R("ff", 0, 1), 0.9); ms(R("lv", 0, 1), -1.0)
+
+    ts(R("nzi"), R("lsi"), 0xFFF00, A.bitwise_and)
+    ts(R("nz"), R("nzi"), 31.0, A.mult, C(0), A.add)
+    tt(R("nu"), R("nz"), R("lsi"), A.add)
+    mm([(R("p2", 0, 128), R("nu"), R("pls"), True, True)])
+    act(R("l0"), R("p2", 0, 128))
+    cp(R("n0"), R("fpi"))
+    ts(R("pxh"), R("pxi"), 0xFFF00, A.bitwise_and)
+    for k in range(2):
+        ts(R("p%d" % (5 + k), 0, 288), R("pxh", 288 * k, 288 * k + 288), 31.0, A.mult, C(1), A.add)
+        tt(R("pk", 288 * k, 288 * k + 288), R("p%d" % (5 + k), 0, 288), R("pxi", 288 * k, 288 * k + 288), A.add)
+    cp(R("omf"), R("omi"))
+    for v in range(NV):
+        tt(R("omx", 128 * v, 128 * v + 128), G(R("omf"), R("oc", 8 * v, 8 * v + 8)), R("dg", 0, 128), A.mult)
+    mm([(R("p7", 8 * v, 8 * v + 8), R("omx", 128 * v, 128 * v + 128), R("blk"), True, True) for v in range(NV)])
+    act(R("nb"), R("p7", 0, 32), 4096.0)
+
+    def sort16(lo, hi, split, dst):
+        for k in range(3):
+            o = "ma" if k != 1 else "mb"
+            if k == split:
+                for h, (on, oc) in enumerate((("p0", 448), (o, 64))):
+                    x, y = R(lo[0], lo[1] + 32 * h, lo[1] + 32 * h + 32), R(hi[0], hi[1] + 32 * h, hi[1] + 32 * h + 32)
+                    tt(R(on, oc, oc + 64, 2), x, y, A.min); tt(R(on, oc + 1, oc + 64, 2), x, y, A.max)
+                lo, hi = ("p0", 448), (o, 64)
+            else:
+                x, y = R(lo[0], lo[1], lo[1] + 64), R(hi[0], hi[1], hi[1] + 64)
+                tt(R(o, 0, 128, 2), x, y, A.min); tt(R(o, 1, 128, 2), x, y, A.max)
+                lo, hi = (o, 0), (o, 64)
+        for h in range(2):
+            tt(R(dst, h, 128, 4), R("ma", 32 * h, 32 * h + 32), R("ma", 64 + 32 * h, 96 + 32 * h), A.min)
+            tt(R(dst, 2 + h, 128, 4), R("ma", 32 * h, 32 * h + 32), R("ma", 64 + 32 * h, 96 + 32 * h), A.max)
+
+    def front(v):
+        b = str(v & 1)
+        gather(SIDE[0] if v else "v", R("pe"), G(R("pk"), R("n%d" % v)))
+        mm([(R("p4", 0, 128), R("pe"), R("ppx"), True, True)])
+        for q in range(4):
+            tt(R("mm", 2 * q, 256, 8), R("l%d" % v, 32 * q, 32 * q + 32), R("p4", 32 * q, 32 * q + 32), A.min)
+            tt(R("mm", 2 * q + 1, 256, 8), R("l%d" % v, 32 * q, 32 * q + 32), R("p4", 32 * q, 32 * q + 32), A.max)
+        lo, hi = ("mm", 0), ("mm", 128)
+        for k in range(3):
+            olo, ohi = ("p0", 128 * (k & 1)), ("ma" if k & 1 else "mb", 0)
+            for h, o in ((0, olo), (1, ohi)):
+                x, y = R(lo[0], lo[1] + 64 * h, lo[1] + 64 * h + 64), R(hi[0], hi[1] + 64 * h, hi[1] + 64 * h + 64)
+                tt(R(o[0], o[1], o[1] + 128, 2), x, y, A.min)
+                tt(R(o[0], o[1] + 1, o[1] + 128, 2), x, y, A.max)
+            lo, hi = olo, ohi
+        x, y = R(lo[0], lo[1], lo[1] + 128), R(hi[0], hi[1], hi[1] + 128)
+        tt(R("ki", 0, 256, 2), x, y, A.min); tt(R("ki", 1, 256, 2), x, y, A.max)
+        ts(R("xi"), R("ki"), 0x10FF, A.bitwise_and)
+        ts(R("zs"), R("ki"), 13, A.arith_shift_right)
+        cp(R("xf"), R("xi"))
+        un(SIDE[3], R("yf"), R("xf"), -2.0, 8192.0)
+        if v < NV - 1 and SIDE[4] == "s":
+            ts(R("p0", 256, 512), R("zs"), -1.0, A.mult)
+            tt(R("zc"), R("p0", 256, 512), R("cz"), A.add)
+            act(R("slb"), R("zc"), -1.0 / 256, 136 - 127.5 / 256 + (2047 + 255.0 / 256) / 256)
+        else:
+            if v < NV - 1:
+                ts(R("p0", 256, 512), R("zs"), -1.0, A.mult)
+                tt(R("zc"), R("p0", 256, 512), R("cz"), A.add)
+            ts(R("slb"), R("zs"), 1.0 / 256, A.mult, 136 - 127.5 / 256, A.add)
+        scan(R("af"), R("yf"), R("xf"), 0.0, A.max, A.min)
+        scan(R("bf"), R("yf"), R("xf"), 4096.0, A.min, A.max)
+        for t, (src, bank) in enumerate((("af", "p2"), ("bf", "p3"))):
+            mm([(R(bank, 128 * h, 128 * h + 128), R(nm, h, 256, 2), R(idn), st, not st)
+                for h in range(2) for nm, idn, st in (("slb", "idb", True), (src, "id16", False))])
+            o = ("oa", "ob")[t] + b
+            ts(R(o, 0, 128), R(bank, 0, 128), C(5 + t), A.add, C(7), A.max)
+            ts(R(o, 128, 256), R(bank, 128, 256), -128.0 - 65536.0 * t, A.add, 0.0, A.max)
+        k = 0
+        for h in range(2):
+            for hf in range(2):
+                for t in "ab":
+                    gather(SG[v][k], R("s" + t + b, 2048 * hf + h, 2048 * hf + 2048, 2),
+                           G(R("tsg"), R("o" + t + b, 128 * h + 64 * hf, 128 * h + 64 * hf + 64)))
+                    k += 1
+            mm([(R("p3", s, 512, 32), R("s" + t + b, s, 4096, 32),
+                 R("rh", 32, 48) if s == 0 else R("rh", 0, 16) if t == "a" else R("rh", 16, 32), t == "a", t == "b")
+                for s in range(h, 32, 2) for t in "ab"])
+        if v < NV - 1:
+            tt(R("ln", 0, 255), R("p0", 256, 511), R("zs", 1, 256), A.add)
+        else:
+            tt(R("ln", 0, 255), R("zs", 1, 256), R("zs", 0, 255), A.subtract)
+        ts(R("ln", 31, 256, 32), R("zs", 31, 256, 32), -1.0, A.mult, 2048.0, A.add)
+        ms(R("ln", 0, 256, 32), -1048576.0)
+        act(R("rst0", 0, 256, 32), R("nb", 8 * v, 8 * v + 8))
+        if v < NV - 1:
+            mm([(R("p2", 256, 512), R("idc"), R("oneb", 0, 256), True, False), (R("p2", 256, 512), R("idp"), R("bf"), False, False),
+                (R("p2", 256, 512), R("idn"), R("af"), False, True)])
+            mm([(R("p4", 256, 512), R("idc"), R("oneb", 0, 256), True, False), (R("p4", 256, 512), R("idb"), R("oneb", 256, 512), False, False),
+                (R("p4", 256, 512), R("idp"), R("bf"), False, False), (R("p4", 256, 512), R("idp"), R("af"), False, True)])
+
+    def seen(v):
+        b = str(v & 1)
+        tt(R("nw"), R("p3", 0, 256), R("ln"), A.mult)
+        scan(R("p0", 256, 512), R("nw"), R("rst0"), 0.0, A.add, A.max)
+        tt(R("lv", 1, 256), R("p0", 256, 511), R("ln", 1, 256), A.min)
+        mm([(R("p2", 128 * h, 128 * h + 128), R("lv", h, 256, 2), R("id32"), True, True) for h in range(2)])
+        tag[0] = "n%d" % v if OLN else "f%da" % v
+        ts(R("lh" + b, 0, 128), R("p2", 0, 128), C(8), A.max)
+        cp(R("lh" + b, 128, 256), R("p2", 128, 256))
+        tt(R("lh" + b, 256, 512), R("p2", 0, 256), R("lh" + b, 0, 256), A.subtract)
+        for hf in range(2):
+            x, y = R("sa" + b, 2048 * hf, 2048 * hf + 2048), R("sb" + b, 2048 * hf, 2048 * hf + 2048)
+            dma("g", x[0], y[0], [x, y], [x], 1 << 19, accum_op=A.add)
+
+    def remake(v):
+        if SIDE[5] == "s":
+            act(R("tc"), R("p3", 256, 512), 1.0, -0.5, ACT.Sign)
+        else:
+            ts(R("e1"), R("p3", 256, 512), 0.0, A.is_gt, 2.0, A.mult)
+            ts(R("tc"), R("e1"), -1.0, A.add)
+        tt(R("nm"), R("p2", 256, 512), R("tc"), A.mult)
+        tt(R("p0", 0, 256), R("p4", 256, 512), R("nm"), A.add)
+        if SIDE[6] == "s":
+            act(R("den"), R("lv"), -8192.0, 8192.0, ACT.Relu)
+        else:
+            ts(R("den"), R("lv"), 0.0, A.is_le, 8192.0, A.mult)
+        tt(R("xa"), R("p0", 0, 256), R("den"), A.subtract)
+        tt(R("p0", 256, 512), R("zc"), R("p0", 0, 256), A.subtract)
+        scan(R("ff", 1, 257), R("den"), R("xa"), 0.9, A.min, A.max)
+        tt(R("xb"), R("p0", 256, 512), R("den"), A.add)
+        scan(R("zz"), R("rstb"), R("xb"), 0.0, A.max, A.min)
+        tag[0] = "n%d" % v
+        ts(R("n8"), R("ff", 32, 257, 32), 1024.0, A.mult)
+        tt(R("t8"), R("zz", 31, 256, 32), R("ff", 32, 257, 32), A.add)
+        ts(R("q8"), R("t8"), -1.0 / 1024, A.mult, (4095 + 255.0 / 256 - 511.5) / 1024, A.add)
+        tt(R("nam"), R("n8"), R("q8"), A.add)
+        tt(R("nx"), G(R("nam"), R("oc", 32, 41)), R("dg", 0, 144), A.mult)
+        mm([(R("p3", 0, 8), R("nx", 16, 144), R("blk"), True, True), (R("p3", 8, 16), R("nx", 0, 128), R("blk"), True, True)])
+        ts(R("nown"), R("p3", 0, 8), C(9), A.add)
+        ts(R("m%d" % v), R("p3", 8, 16), C(10), A.add)
+        send(R("m%d" % v), R("n%d" % (v + 1)), "rn%d" % v, 2048)
+        if SIDE[1] == "v":
+            ts(R("te"), G(R("pk"), R("nown")), -4352.0, A.add)
+        else:
+            act(R("te"), G(R("pk"), R("nown")), 1.0, -4352.0)
+        mm([(R("p4", 128, 256), R("te"), R("ptl"), True, True)])
+        tag[0] = "r%d" % v
+        un(SIDE[2], R("thr"), R("t8"), -8192.0, 16785376.0)
+        gather(SIDE[2], R("thb"), G(R("thr"), R("oc", 48, 56)))
+        tt(R("p0", 0, 256), R("ff", 1, 257), R("ff", 0, 256), A.is_equal)
+        ts(R("nm"), R("p0", 0, 256), -M1, A.mult, M1, A.add)
+        tt(R("tc"), R("p0", 0, 256), R("sc"), A.mult)
+        tt(R("vh"), R("p0", 256, 512), R("nm"), A.min)
+        scan(R("p0", 0, 256), R("rstm"), R("nm"), 0.0, A.min, A.add)
+        tt(R("ei"), R("p0", 0, 256), R("tc"), A.add)
+        ts(R("e1"), R("ei"), 0x8888, A.bitwise_and)
+        ts(R("e2"), R("e1"), M2, A.mult)
+        ts(R("e3"), R("e2"), 0xF000, A.bitwise_and)
+        tt(R("p0", 0, 128), R("e3", 0, 256, 2), R("vh", 0, 256, 2), A.add)
+        tt(R("ta"), R("e3", 1, 256, 2), R("vh", 1, 256, 2), A.add)
+        e, o = 0, "ta"
+        for k in range(4):
+            e2, o2 = 128 - e, ("tb" if o == "ta" else "ta")
+            for h in range(2):
+                x, y = R("p0", e + h, e + 128, 2), R(o, h, 128, 2)
+                for j, op in enumerate((A.max, A.min)):
+                    tt(R("p0", e2 + 64 * j, e2 + 64 * j + 64) if h == 0 else R(o2, 64 * j, 64 * j + 64), x, y, op)
+            e, o = e2, o2
+        tt(R("p0", 128, 256), R("p0", e, e + 128), R(o), A.max)
+        tt(R("nu"), R("posc"), R("p0", 128, 256), A.subtract)
+        ts(R("nzi"), R("nu"), 111.0 / 256 - 0.7, A.add)
+        ts(R("p0", 0, 128), R("nu"), 256.0, A.mult, -1.0, A.add)
+        ts(R("nz"), R("nzi"), 7936.0, A.mult, -TWO24, A.add)
+        tt(R("nkk"), R("p0", 0, 128), R("nz"), A.add)
+        tt(R("tm"), R("p4", 128, 256), R("thb"), A.is_lt)
+        un(SIDE[7], R("nw1"), R("tm"), KF + TWO24, -TWO24)
+        tt(R("p0", 384, 448), R("p4", 128, 192), R("nw1", 0, 64), A.max)
+        tt(R("nk", 64, 128), R("p4", 192, 256), R("nw1", 64, 128), A.max)
+        sort16(("p0", 384), ("nk", 64), 1, "tm")
+        for q in range(4):
+            tt(R("uu", q, 128, 4), R("tm", 32 * q, 32 * q + 32), R("nkk", q, 128, 4), A.min)
+        sort16(("uu", 0), ("uu", 64), 0, "o%d" % v)
+        send(R("o%d" % v), R("l%d" % (v + 1)), "rl%d" % v, 65536)
+
+    def floats(v):
+        b = str(v & 1)
+        al = "al" + b
+        tag[0] = "f%dc" % v
+        n = 128 // CQ
+        for q in range(CQ):
+            for h in range(2):
+                for t in "ab":
+                    gather(CO[v][4 * (2 * q // CQ) + 2 * h + (t == "b")], R("c" + t + b, 32 * n * q + h, 32 * n * (q + 1), 2),
+                           G(R("tco"), R("o" + t + b, 128 * h + n * q, 128 * h + n * (q + 1))))
+        tag[0] = "f%da" % v
+        n = 128 // AH[v]
+        k = 0
+        for q in range(AH[v]):
+            for s0 in range(0, 32, 512 // n):
+                bank = "p" + BANKA[v][k]; k += 1
+                lst = []
+                for j in range(512 // n):
+                    h, r = (s0 + j) >> 4, (s0 + j) & 15
+                    for part in range(1 if s0 + j == 0 else 2):
+                        a = 256 * part + 128 * h + n * q
+                        lst.append((R(bank, n * j, n * j + n), R("sel", 128 * r, 128 * r + 128), R("lh" + b, a, a + n),
+                                    part == 0, part == 1 or s0 + j == 0))
+                mm(lst)
+                for j in range(512 // n):
+                    h, r = (s0 + j) >> 4, (s0 + j) & 15
+                    tt(R(al, 2048 * h + 16 * n * q + r, 2048 * h + 16 * n * (q + 1), 16), R(bank, n * j, n * j + n),
+                       R("sa" + b, 32 * n * q + 2 * r + h, 32 * n * (q + 1), 32), A.mult)
+        tag[0] = "f%do" % v
+        for c in range(8):
+            q, h = c >> 1, c & 1
+            un(OM[v][c], R("om" + b, 1024 * q + h, 1024 * q + 1024, 2), R(al, 2048 * h + 512 * q, 2048 * h + 512 * q + 512), -2.0 ** -17, 1.0)
+        tag[0] = "f%du" % v
+        for c in range(8):
+            bank = "p" + BANKS[v][c]; a = 512 * c
+            mm([(R(bank), R("idb"), R("ca" + b, a + 1, a + 513), True, False), (R(bank), R("idb"), R("cb" + b, a + 1, a + 513), False, False),
+                (R(bank), R("nidb"), R("ca" + b, a, a + 512), False, False), (R(bank), R("nidb"), R("cb" + b, a, a + 512), False, True)])
+            scan(R("ub", a, a + 512, -1), R(bank, 0, 512, -1), R("om" + b, a, a + 512, -1), 0.0, A.add, A.mult)
+        tag[0] = "f%dy" % v
+        for hf in range(2):
+            a = 1024 * hf
+            ns = 32
+            if FOLD[v][hf] == "d":
+                ns = 16
+                x, y = R(al, a, a + 1024), R(al, 2048 + a, 3072 + a)
+                dma("g", x[0], y[0], [x, y], [x], 1 << 19, accum_op=A.add)
+            for s0 in range(0, ns, 4):
+                mm([(R("p7", 128 + 64 * hf, 192 + 64 * hf), R("id32"), R(al, 2048 * (s >> 4) + a + (s & 15), 2048 * (s >> 4) + a + 1024, 16),
+                     s == 0, s == ns - 1) for s in range(s0, s0 + 4)])
+        mm([(R("p7", 0, 128), R("idb"), R("ca" + b, 1, 4096, 32), True, False), (R("p7", 0, 128), R("idb"), R("cb" + b, 1, 4096, 32), False, False),
+            (R("p7", 0, 128), R("id32"), R("ub", 1, 4096, 32), False, True)])
+        act(R("yo" + b, 128, 256), R("p7", 128, 256), 2.0 ** -14, -8.0)
+        act(R("yo" + b, 0, 128), R("p7", 0, 128))
+        dma("y", T.yt[:, 128 * v:128 * v + 128], R("yo" + b, 128, 256)[0], [R("yo" + b, 128, 256)], [], 65536)
+        dma("y", T.yc[:, 128 * v:128 * v + 128], R("yo" + b, 0, 128)[0], [R("yo" + b, 0, 128)], [], 65536)
+
+    for v in range(NV):
+        tag[0] = "m%d" % v
+        front(v)
+        tag[0] = "s%d" % v
+        seen(v)
+        if v < NV - 1:
+            tag[0] = "r%d" % v
+            remake(v)
+        floats(v)
+
+    n = len(ops)
+    before = [sorted(o["d"] | o["o"]) for o in ops]
+    after = [[] for _ in range(n)]
+    for i in range(n):
+        for d in before[i]:
+            after[d].append(i)
+
+    def sched(pr):
+        left = [len(x) for x in before]
+        rdy = [0.0] * n
+        free = {e: 0.0 for e in "vspgyr"}
+        cand = {e: [] for e in free}
+        sq = {e: [] for e in free}
+        gl = []; fin = [0.0] * n
+        for i in range(n):
+            if left[i] == 0:
+                cand[ops[i]["e"]].append(i)
+        done = set()
+        nxc = {e: [i for i in range(n) if ops[i]["e"] == e and ops[i]["t"][0] in "msrn"] for e in free}
+        while len(done) < n:
+            best = None
+            for e in cand:
+                if not cand[e]:
+                    continue
+                t0 = max(free[e], min(rdy[i] for i in cand[e]))
+                i = max((i for i in cand[e] if rdy[i] <= t0), key=lambda j: pr[j])
+                soon = [j for j in cand[e] if rdy[j] <= t0 + LOOK * ops[i]["c"] and pr[j] > pr[i] + 3000 and ops[i]["c"] > 300]
+                if soon:
+                    i = min(soon, key=lambda j: rdy[j])
+                t = max(free[e], rdy[i])
+                if best is None or t < best[0]:
+                    best = (t, e, i)
+            t, e, i = best
+            if ops[i]["t"][0] == "f" and ops[i]["c"] > 300:
+                memo = {}
+
+                def est(j, depth):
+                    if j not in memo:
+                        x = max(rdy[j], t)
+                        if left[j]:
+                            x = 1e18 if depth == 0 else max([x] + [est(d, depth - 1) + ops[d]["c"] + ops[d]["l"] + LAT for d in before[j] if d not in done])
+                        memo[j] = max(x, free[ops[j]["e"]]) if ops[j]["e"] != e else x
+                    return memo[j]
+                while nxc[e] and nxc[e][0] in done:
+                    nxc[e].pop(0)
+                x = min([est(j, 8) for j in nxc[e][:4] if j not in done] + [1e18])
+                if t < x < t + HOLD[e] * ops[i]["c"]:
+                    fit = [j for j in cand[e] if rdy[j] <= t and ops[j]["c"] <= x - t + 60]
+                    if fit:
+                        i = max(fit, key=lambda j: pr[j])
+                    else:
+                        free[e] = x
+                        continue
+            done.add(i)
+            cand[e].remove(i); sq[e].append(i); gl.append(i)
+            free[e] = t + ops[i]["c"]
+            fin[i] = free[e] + ops[i]["l"]
+            for j in after[i]:
+                if i in ops[j]["d"] or e != ops[j]["e"]:
+                    rdy[j] = max(rdy[j], fin[i] + LAT)
+                left[j] -= 1
+                if left[j] == 0:
+                    cand[ops[j]["e"]].append(j)
+        return max(fin), sq, gl, fin
+
+    if "plan" not in PLAN:
+        pr = [0.0] * n
+        for i in range(n - 1, -1, -1):
+            pr[i] = ops[i]["c"] + ops[i]["l"] + max([pr[j] + LAT for j in after[i]] + [0.0])
+        for i, o in enumerate(ops):
+            t = o["t"]
+            if t[0] == "f":
+                pr[i] = 1e6 + 1000.0 * URG[t[2]][int(t[1])] - i
+            elif t[0] == "n":
+                pr[i] += 2e6
+            else:
+                pr[i] += 1e6 + (1e6 if t == "k" and o["e"] != "g" and o["c"] < 100 else 0.0)
+        PLAN["plan"] = sched(pr)
+    PLAN["ops"] = ops
+    seq, glob = PLAN["plan"][1:3]
+    gpos = {i: k for k, i in enumerate(glob)}
+
+    esem = {"v": "sv", "s": "ss", "p": "sp", "g": "sgq"}
+    place = {}
+    for e in seq:
+        for k, i in enumerate(seq[e]):
+            place[i] = k + 1
+    know = {e: {} for e in seq}
+    snap = {}
+    waits = {}
+    need = set()
+    for i in glob:
+        o = ops[i]; e = o["e"]; kn = know[e]; want = {}
+        for d in o["d"]:
+            key, val = (ops[d]["sem"][0], 1) if ops[d]["sem"] else (ops[d]["e"], place[d])
+            if val > want.get(key, (0, 0))[0]:
+                want[key] = (val, d)
+        w = []
+        for key, (val, d) in sorted(want.items(), key=lambda x: -gpos[x[1][1]]):
+            if kn.get(key, 0) >= val:
+                continue
+            w.append(d); need.add(d); kn[key] = val
+            for k2, v2 in snap[d].items():
+                if v2 > kn.get(k2, 0):
+                    kn[k2] = v2
+        waits[i] = w
+        snap[i] = dict(kn)
+    cnt = {e: 0 for e in esem}
+    val = {}
+    for e in esem:
+        for i in seq[e]:
+            if i in need and not ops[i]["sem"]:
+                cnt[e] += 1; val[i] = cnt[e]
+    for i in glob:
+        o = ops[i]; e = o["e"]
+        if e == "r":
+            continue
+        for d in waits[i]:
+            if ops[d]["sem"]:
+                Q[e].wait_ge(T.sem[ops[d]["sem"][0]], ops[d]["sem"][1])
+            else:
+                Q[e].wait_ge(T.sem[esem[ops[d]["e"]]], val[d])
+        r = o["f"]()
+        if i in val:
+            r.then_inc(T.sem[esem[e]], 1)
+    for i in glob:
+        if ops[i]["sem"] and i not in need:
+            g.wait_ge(T.sem[ops[i]["sem"][0]], ops[i]["sem"][1])

@@ -13,48 +13,53 @@ def _s(names, n, d):
 
 
 _s("tsg tco", WT, B)
-_s("pxi pxh", 576, I); _s("pk", 576, F); _s("lsi", 128, I)
-_s("fpi", 8, I); _s("omi", 32, I); _s("omf nb", 32, F); _s("omx", 512, F)
+_s("pxi", 576, I); _s("tn pxh", 576, F); _s("lsi pg ea ec", 128, I)
+_s("fpi", 8, I); _s("omi", 32, I); _s("omf nb", 32, F); _s("omx omy", 128, F)
 _s("sel", 2048, B)
-_s("ones id32 id16 ppx pls ptl posc idp idn", 128, F); _s("idb nidb idc", 128, B)
-_s("dgi", 144, I); _s("dg", 144, F); _s("blk", 8, F); _s("rh", 48, B)
-_s("pid", 8, I); _s("col", 16, F); _s("oci", 64, I); _s("oc", 64, U)
-_s("rst0 rstm rstb sc cz", 256, F); _s("oneb", 512, B)
-_s("l0 l1 l2 l3 o0 o1 o2", 128, F); _s("n0 n1 n2 n3 m0 m1 m2 nown", 8, U)
-_s("pe te ma mb", 128, F); _s("mm", 256, F)
-_s("ki xi zs ei e1 e2 e3", 256, I)
-_s("xf yf af bf ln zc nw lv den xa xb zz nm tc vh", 256, F); _s("ff", 264, F); _s("slb", 256, B)
+_s("ones id32 idl idz", 128, F); _s("ppx pls posc", 64, F); _s("idb nidb idh nidh idm", 128, B)
+_s("dgi", 144, I); _s("dg", 144, F); _s("blk bl4", 8, F); _s("rh", 64, B)
+_s("pid", 8, I); _s("col", 16, F); _s("oci", 32, I); _s("oc", 32, U)
+_s("rst", 256, F); _s("rstm", 192, F); _s("c44 c100", 128, B); _s("c1", 64, B); _s("ct", 256, B)
+_s("l0 l1 l2 l3 o0 o1", 128, F); _s("n0 n1 n2 n3", 16, U); _s("nm0 nm1", 32, U)
+_s("eb pe te hp hb hl mc thb", 128, F)
+_s("ma mb hh ln nw lv tc nm zz zc", 256, F); _s("rr ff", 272, F); _s("xf yf af bf slb den", 256, B)
+_s("n2m tq yy", 384, F); _s("ei e1 e2", 384, I); _s("ta tb", 192, F)
+SCRATCH["live"] = ("sbuf", [128, 8, 48], F)
 _s("oa0 oa1 ob0 ob1", 256, U); _s("lh0 lh1", 512, B)
-_s("t8 n8 nam thr", 8, F); _s("q8", 8, I); _s("nx", 144, F)
-_s("thb tm ta tb nk nu nw1 nz nkk uu", 128, F); _s("nzi", 128, I)
-_s("sa0 sa1 sb0 sb1", 4096, B); _s("ca0 ca1 cb0 cb1", 4112, B)
+_s("nam t8", 16, F); _s("q8 e8 n8", 8, I); _s("nx", 288, F)
+_s("sb ss0 ss1", 4096, B); _s("ca0 ca1 cb0 cb1", 4128, B); _s("cc0 cc1", 4128, "float16"); _s("idf nidf", 128, "float16")
 _s("al0 al1 ub om0 om1", 4096, F); _s("yo0 yo1", 256, F)
 for _k in range(8):
     SCRATCH["p%d" % _k] = ("psum", [128, 512], F)
-NDS = 48
-SEMAPHORES = ["sv", "ss", "sp", "sgq"] + ["d%d" % k for k in range(NDS)] + ["rn0", "rn1", "rn2", "rl0", "rl1", "rl2"]
+SCRATCH["p1"] = ("psum", [128, 8, 64], F)
+NDS = 64
+SEMAPHORES = ["sv", "ss", "sp", "sgq"] + ["d%d" % k for k in range(NDS)] + [x + str(k) for x in ("rn", "rl") for k in range(6)]
 
 A = AluOpType
 ACT = ActivationFunctionType
-M1, M2 = 33825.0, 585.0
-TWO24 = 16777216.0
-KF = 2047 * 8192.0 + 3840.0
+UN = 2.0 ** -20
+M1, MASK, M2 = 266305.0, 0x42108, 4369 * 2.0 ** -15
+R256, R512 = 2.0 ** 11, 1.5 * 2.0 ** 12
 
-CY, PCY, GA, LAT = 1.0, 0.5, 1.56, 90.0
-DL, DR, RL, RR = 1800.0, 200.0, 1500.0, 60.0
-SG = ['vvsvsssv', 'sssvvsvs', 'svvssvss', 'svsvsvsv']
-CO = ['sssvsssv', 'ssssssss', 'ssssssss', 'sssvssvs']
-OM = ['ssvsssvs', 'ssssssvv', 'ssssssss', 'svsssvss']
-SIDE = 'sssssssv'
-FOLD = ['dd', 'pd', 'dd', 'dd']
-AH = [2, 2, 2, 1]
-CQ = 4
-OLN = 1
-BANKA = ['15151515', '15151515', '15615615', '14321432']
-BANKS = ['56156156', '65165165', '65165165', '56143256']
-URG = {'c': [52, 0, -8, -68], 'a': [68, 34, 30, -172], 'o': [49, 10, 15, -84], 'u': [60, 34, 4, -80], 'y': [34, 30, -41, -64]}
-HOLD = {'v': 0.3, 's': 0.7, 'p': 0.8, 'g': 1.0, 'y': 0.0}
-LOOK = 0.2
+CY, PCY, GA, LAT, XLAT, PLAT = 0.95, 0.5, 1.9, 240.0, 170.0, 100.0
+DL, DR, DA, DF, RN, RL = 1800.0, 300.0, 2000.0, 4000.0, 4000.0, 2000.0
+SG = ['f'] * 8
+CM = 'ssssssff'
+CO = ['ssssssss'] * 8
+OM = ['ssss'] * 8
+FOLD = '22222111'
+SIDE = 'sssssv'
+SPLIT = 'fsnrj'
+CQ, UQ = 2, 128
+SQ = [[32, 32], [32, 16, 16]]
+BANKA = ['56'] * 6 + ['50', '52']
+BANKS = ['6'] * 6 + ['63', '64']
+BANKL = '55555555'
+BANKO = ['77'] * 6 + ['70', '22']
+URG = {'k': 0, 'c': 10, 'a': 10, 'o': 10, 'u': 15, 'y': 10}
+STAG = 4.0
+HOLD = {'v': 0.17, 's': 0.71, 'p': 0.51, 'g': 0.62, 'y': 0.58, 'r': 0.0}
+PASSES, AHEAD = 6, 1000.0
 PLAN = {}
 
 
@@ -72,15 +77,27 @@ def rank_program(g, core, T, topo):
     nd = [0]
     tag = ["k"]
 
-    def R(name, a=0, b=None, st=1):
+    def cells(c, p):
+        return np.concatenate([2 * c, 2 * c + 1]) if p is None else 2 * c + p
+
+    def R(name, a=0, b=None, st=1, p=None):
         if b is None:
             b = SCRATCH[name][1][1]
-        if st > 0:
-            return (T[name][:, a:b:st] if st > 1 else T[name][:, a:b], name, np.arange(a, b, st))
-        return (T[name][:, b - 1:(a - 1 if a > 0 else None):-1], name, np.arange(a, b))
+        rows = slice(0, 128) if p is None else slice(64 * p, 64 * p + 64)
+        c = np.arange(a, b, abs(st))
+        cs = slice(a, b, st) if st > 1 else slice(a, b) if st > 0 else slice(b - 1, a - 1 if a > 0 else None, -1)
+        return (T[name][rows, cs], name, cells(c, p), len(c))
+
+    def R3(name, g0, a, b, st=1, ng=4):
+        sh = SCRATCH[name][1][1:]
+        c = np.arange(sh[0] * sh[1]).reshape(sh)[g0:g0 + ng, a:b:st].ravel()
+        return (T[name][:, g0:g0 + ng, a:b:st], name, cells(c, None), len(c))
+
+    def parts(step):
+        return ((0, 2), (2, 2)) if step in SPLIT else ((0, 4),)
 
     def G(win, off):
-        return (win[0].indirect(off[0]), win[1], win[2], off)
+        return (win[0].indirect(off[0]), win[1], win[2], win[3], off)
 
     def add(eng, fn, reads, writes, cost, lat=0.0, sem=None):
         me = len(ops); deps = set(); order = set()
@@ -88,12 +105,12 @@ def rank_program(g, core, T, topo):
         for r in reads:
             if isinstance(r, tuple):
                 rs.append(r)
-                if len(r) == 4:
-                    rs.append(r[3])
+                if len(r) == 5:
+                    rs.append(r[4])
         for r in rs + writes:
             nme = r[1]
             if nme not in wr:
-                wr[nme] = np.full(SCRATCH[nme][1][1], -1); rd[nme] = []
+                wr[nme] = np.full(2 * int(np.prod(SCRATCH[nme][1][1:])), -1); rd[nme] = []
             if SCRATCH[nme][0] == "psum":
                 e = ep.setdefault(nme, [eng, [], []])
                 if e[0] != eng:
@@ -133,27 +150,31 @@ def rank_program(g, core, T, topo):
         return SCRATCH[x[1]][0] == "psum"
 
     def vc(o, i, k=1.0):
-        n = len(o[2])
-        return 50 + n * GA * CY if len(i) == 4 else max(64, n * k) * CY
+        return 50 + o[3] * GA * CY if len(i) == 5 else max(64, o[3] * k) * CY
+
+    def half(*x):
+        return 0.5 if all(SCRATCH[y[1]][2] in (B, U) for y in x) else 1.0
 
     def tt(o, a, b, op):
         return add("v", lambda: g.vector.tensor_tensor(o[0], a[0], b[0], op), [a, b], [o], vc(o, a, 1.0 if ps(a) or ps(b) else 2.0))
 
     def ts(o, a, s1, op0, s2=None, op1=None):
         if op1 is None:
-            return add("v", lambda: g.vector.tensor_scalar(o[0], a[0], ap(s1), None, op0), [a, s1], [o], vc(o, a))
-        return add("v", lambda: g.vector.tensor_scalar(o[0], a[0], ap(s1), ap(s2), op0, op1), [a, s1, s2], [o], vc(o, a))
+            return add("v", lambda: g.vector.tensor_scalar(o[0], a[0], ap(s1), None, op0), [a, s1], [o], vc(o, a, half(o, a)))
+        return add("v", lambda: g.vector.tensor_scalar(o[0], a[0], ap(s1), ap(s2), op0, op1), [a, s1, s2], [o], vc(o, a, half(o, a)))
 
     def cp(o, a):
-        return add("v", lambda: g.vector.tensor_copy(o[0], a[0]), [a], [o], vc(o, a))
+        return add("v", lambda: g.vector.tensor_copy(o[0], a[0]), [a], [o], vc(o, a, half(o, a)))
 
     def ms(o, c):
-        return add("v", lambda: g.vector.memset(o[0], c), [], [o], max(64, len(o[2])) * CY)
+        return add("v", lambda: g.vector.memset(o[0], c), [], [o], vc(o, o, half(o)))
 
     def scan(o, a, b, init, op0, op1):
-        return add("v", lambda: g.vector.tensor_tensor_scan(o[0], a[0], b[0], init, op0, op1), [a, b], [o], vc(o, a))
+        return add("v", lambda: g.vector.tensor_tensor_scan(o[0], a[0], b[0], init, op0, op1), [a, b], [o], vc(o, a, half(o, a, b)))
 
     def act(o, a, scale=1.0, bias=0.0, fn=ACT.Copy):
+        if isinstance(scale, tuple):
+            return add("s", lambda: g.scalar.activation(o[0], a[0], fn, scale=scale[0]), [a, scale], [o], vc(o, a) + 15)
         if bias == 0.0 and scale == 1.0:
             return add("s", lambda: g.scalar.activation(o[0], a[0], fn), [a], [o], vc(o, a) + 15)
         return add("s", lambda: g.scalar.activation(o[0], a[0], fn, bias=bias, scale=scale), [a], [o], vc(o, a) + 15)
@@ -176,343 +197,388 @@ def rank_program(g, core, T, topo):
             for o, l, x, a, b in lst:
                 r = g.tensor.matmul(o[0], l[0], x[0], a, b)
             return r
-        c = sum(max(64, len(x[2])) * (4 if SCRATCH[x[1]][2] == F else 1) for o, l, x, a, b in lst) * PCY
-        return add("p", fn, [q[1] for q in lst] + [q[2] for q in lst], [q[0] for q in lst], c, 60.0)
+        c = sum(max(64, x[3]) * (4 if SCRATCH[x[1]][2] == F else 1) for o, l, x, a, b in lst) * PCY
+        return add("p", fn, [q[1] for q in lst] + [q[2] for q in lst], [q[0] for q in lst], c, PLAT)
+
+    def grp(o, terms):
+        return [(o, l, x, k == 0, k == len(terms) - 1) for k, (l, x) in enumerate(terms)]
 
     def iota(o, pat, base, cm):
         if SCRATCH[o[1]][2] == I:
             fn = lambda: g.iota(o[0], pat, base, cm)
         else:
             fn = lambda: g.iota(o[0], pat, base, cm, allow_small_or_imprecise_dtypes=True)
-        return add("g", fn, [], [o], 130 + 2 * len(o[2]) * CY)
+        return add("g", fn, [], [o], 130 + 2 * o[3] * CY)
 
     def asel(o, a, pat, base):
-        return add("g", lambda: g.affine_select(o[0], a[0], pat, A.is_equal, 0.0, base, -1), [a], [o], 170 + 2 * len(o[2]) * CY)
+        return add("g", lambda: g.affine_select(o[0], a[0], pat, A.is_equal, 0.0, base, -1), [a], [o], 170 + 2 * o[3] * CY)
 
     def newsem():
         nd[0] += 1
         return "d%d" % (nd[0] - 1)
 
-    def dma(eng, o, i, reads, writes, nbytes, **kw):
+    def dma(eng, o, i, reads, writes, nbytes, more=0.0, **kw):
         s = newsem()
         return add(eng, lambda: Q[eng].dma_start(o, i, **kw).then_inc(T.sem[s], 16), reads, writes,
-                   900.0 if eng == "g" else 60.0, DL + nbytes / DR, (s, 16))
+                   900.0 if eng == "g" else 60.0, DL + more + nbytes / DR, (s, 16))
 
-    def send(src, dst, rs, nbytes):
+    def send(src, dst, rs, wait):
         s = newsem()
         a = add("g", lambda: g.remote_dma(dst[0], src[0], T.sem[rs], T.sem[s], pid, rid, mask), [src], [], 300.0, 1000.0, (s, neng))
-        b = add("r", None, [], [dst], 0.0, RL + nbytes / RR, (rs, neng))
+        b = add("r", None, [], [dst], 0.0, wait, (rs, neng))
         ops[b]["o"].add(a)
 
-    dma("y", R("lsi")[0], T.ls[:], [], [R("lsi")], 65536)
-    dma("s", R("pxi")[0], T.px[:], [], [R("pxi")], 294912)
     dma("y", R("fpi")[0], T.fp[:], [], [R("fpi")], 4096)
-    dma("y", R("tsg", 0, 2304)[0], T.sg[:], [], [R("tsg", 0, 2304)], 589824)
+    dma("s", R("pxi")[0], T.px[:], [], [R("pxi")], 294912)
+    dma("y", R("lsi")[0], T.ls[:], [], [R("lsi")], 65536)
+    dma("y", R("tsg", 0, 2304)[0], T.sg[:], [], [R("tsg", 0, 2304)], 589824, 1500.0)
     dma("s", R("omi")[0], T.om[:], [], [R("omi")], 16384)
-    dma("y", R("tco", 0, 2304)[0], T.co[:], [], [R("tco", 0, 2304)], 589824)
-
-    ms(R("ones"), 1.0)
-    iota(R("pid", 0, 1), [[0, 1]], 0, 1)
-    asel(R("pls"), R("ones"), [[16, 4], [1, 16], [64, 2]], 0)
-    asel(R("ppx"), R("ones"), [[16, 4], [-1, 16], [64, 2]], 15)
-    iota(R("xa"), [[0, 4], [1, 2], [0, 32]], 0, 0)
-    asel(R("id32"), R("ones"), [[1, 128]], 0)
-    iota(R("q8"), [[-16, 8]], 0, 1)
-    iota(R("xb"), [[0, 8], [1, 32]], 0, 0)
-    iota(R("dgi"), [[0, 9], [-1, 16]], 16, 1)
-    iota(R("oci", 0, 32), [[1, 32]], 0, 0)
-    iota(R("oci", 32, 42), [[1, 10]], 7, 0)
-    iota(R("oci", 48, 56), [[0, 8]], 0, 1)
-    asel(R("ptl"), R("ones"), [[1, 16], [16, 8]], 0)
-    for q in range(4):
-        iota(R("posc", 32 * q, 32 * q + 32), [[-16384, 2], [-32768, 2], [0, 8]], (16 - (q >> 1) - 2 * (q & 1)) * 4096, 0)
-    act(R("sel"), R("tsg", 0, 2048), 0.0, 1.0)
-    tag[0] = "f0a"
-    asel(R("sel"), R("sel"), [[1, 16], [16, 8], [0, 16]], 0)
-    tag[0] = "k"
+    dma("y", R("tco", 0, 2304)[0], T.co[:], [], [R("tco", 0, 2304)], 589824, 4000.0)
 
     def C(k):
         return R("col", k, k + 1)
 
     def P(k):
         return R("pid", k, k + 1)
+    ms(R("ones"), 1.0); ms(R("hl", 0, 64), UN)
+    asel(R("pls", p=0), R("hl", 0, 64, p=0), [[1, 16], [16, 4]], 0)
+    asel(R("ppx", p=0), R("hl", 0, 64, p=0), [[-1, 16], [16, 4]], 15)
+    act(R("pls", p=1), R("pls", p=0)); act(R("ppx", p=1), R("ppx", p=0))
+    asel(R("id32"), R("ones"), [[1, 128]], 0)
+    iota(R("pid", 0, 1), [[0, 1]], 0, 1)
+    iota(R("q8"), [[-16, 8]], 0, 1)
+    iota(R("oci", 0, 4), [[1, 4]], 0, 0)
+    iota(R("oci", 4, 14), [[1, 10]], 3, 0)
+    iota(R("oci", 16, 18), [[64, 2]], 0, 0)
+    iota(R("dgi"), [[0, 9], [-1, 16]], 16, 1)
+    iota(R("tq", 0, 192), [[0, 4], [1, 48]], -64, 0)
+    for q in range(4):
+        iota(R("yy", 16 * q, 16 * q + 16), [[4, 2], [8, 2], [0, 4]], 1 + (q >> 1) + 2 * (q & 1), 0)
+    act(R("idb"), R("id32")); act(R("idm"), R("id32"), -16.0 / UN)
     ts(P(1), P(0), 15, A.bitwise_and)
-    ts(P(2), P(0), 4, A.arith_shift_right, 1, A.bitwise_and)
-    ts(C(0), P(1), 256.0, A.mult, -TWO24, A.add)
-    ts(C(1), P(1), 256.0, A.mult, 4096.0 - TWO24, A.add)
     ts(C(2), P(1), 0.0, A.is_equal)
-    ts(C(5), C(2), -1048576.0, A.mult, -128.0, A.add)
-    ts(C(6), C(2), -1048576.0, A.mult, -128.0 - 65536.0, A.add)
+    ts(C(5), C(2), -1048576.0, A.mult, 2176.0, A.add)
+    ts(C(6), C(2), -1048576.0, A.mult, -1024.0, A.add)
     ts(C(7), C(2), 2304.0, A.mult)
-    ts(C(8), C(2), 4096.0, A.mult)
-    ts(C(9), P(2), -2.0, A.mult)
-    ts(C(10), P(2), 2.0, A.mult, -2.0, A.add)
-    act(R("id16"), R("id32"), 16.0); act(R("idb"), R("id32")); act(R("nidb"), R("id32"), -1.0)
-    act(R("idp"), R("id32"), 1.0 / 512); act(R("idn"), R("id32"), -1.0 / 512); act(R("idc"), R("id32"), -8.0)
+    ms(R("tsg", 2304, WT), 16.0); ms(R("tco", 2304, WT), 0.0)
     ts(R("q8"), R("q8"), 4, A.arith_shift_right)
     ts(R("blk"), R("q8"), 0.0, A.is_equal)
-    for k, x in enumerate((-4096.0, -1.0, -4096.0, 1.0, 4096.0, 1.0)):
+    ts(R("n8", 0, 4), R("q8", 0, 4), 3, A.bitwise_and)
+    ts(R("bl4", 0, 4), R("n8", 0, 4), 0.0, A.is_equal)
+    ms(R("bl4", 4, 8), 0.0)
+    for k, x in enumerate((2048.0, -1.0, 0.0, 2.0, 2.0 ** 30, 0.0, 2048.0, 1.0)):
         act(R("rh", 8 * k, 8 * k + 8), R("blk"), x)
     ts(R("dgi"), R("dgi"), 15, A.bitwise_and)
     ts(R("dg"), R("dgi"), 0.0, A.is_equal)
-    ts(R("oci", 32, 42), R("oci", 32, 42), 7, A.bitwise_and)
-    ts(R("oci", 48, 56), R("oci", 48, 56), 7, A.bitwise_and)
-    cp(R("oc", 0, 42), R("oci", 0, 42)); cp(R("oc", 48, 56), R("oci", 48, 56))
-    act(R("oneb", 256, 512), R("xa"), 1.0 / 512)
-    act(R("cz"), R("xa"), 1.0 / 512, 2047 + 255.0 / 256)
-    act(R("zz"), R("xb"), fn=ACT.Sign)
-    act(R("rstm"), R("zz"), 4194304.0, -M1)
-    act(R("rstb"), R("zz"), -65536.0, 65536.0)
-    act(R("rst0"), R("zz"), 0.0)
-    act(R("sc"), R("xb"), -M1, 32 * M1)
-    act(R("oneb", 0, 256), R("xb"), 0.0, 1.0)
-    ms(R("tsg", 2304, WT), 16.0); ms(R("tco", 2304, WT), 0.0)
-    for x in ("ca0", "ca1", "cb0", "cb1"):
-        ms(R(x, 4096, 4112), 0.0)
-    ms(R("ff", 0, 1), 0.9); ms(R("lv", 0, 1), -1.0)
+    ms(R("dg", 0, 16, p=0), 0.0); ms(R("dg", 80, 144, p=0), 0.0); ms(R("dg", 16, 80, p=1), 0.0)
+    ts(R("oci", 4, 14), R("oci", 4, 14), 3, A.bitwise_and)
+    ts(P(2), P(0), 12, A.bitwise_and); ts(P(3), P(0), 3, A.bitwise_and); ts(P(4), P(0), 2, A.arith_shift_right, 12, A.bitwise_and)
+    ts(C(8), P(2), 4.0, A.mult); tt(C(9), P(3), P(4), A.add)
+    ts(R("oci", 16, 18), R("oci", 16, 18), C(8), A.add, C(9), A.add)
+    cp(R("oc", 0, 14), R("oci", 0, 14)); cp(R("oc", 16, 18), R("oci", 16, 18))
+    ms(R("rst"), 1.0); ms(R("rr", 0, 272, 136), 1.0); ms(R("ff", 0, 272, 136), 500 * UN)
+    act(R("idh"), R("id32"), 0.5); act(R("nidh"), R("id32"), -0.5); act(R("idz"), R("id32"), -0.5)
+    act(R("idl"), R("id32"), -4096.0);
+    act(R("c1"), R("ones", 0, 64)); act(R("c100"), R("ones"), -100 * UN)
+    mid = 44 if SIDE[1] == "s" else 144
+    act(R("c44"), R("ones"), mid * UN); act(R("c44", 0, 128, 32), R("ones", 0, 4), (mid + 300) * UN)
+    ms(R("ct"), 4096.0); ms(R("ct", 0, 128, 16), 8192.0)
+    act(R("posc"), R("yy", 0, 64), 1.0, 144 * UN)
+    act(R3("p1", 4, 0, 48), R("tq", 0, 192), M1)
+    ms(R("rstm"), -2.0 ** 30); ms(R("rstm", 0, 192, 48), 64 * M1)
+    tag[0] = "fa0"
+    act(R("nidb"), R("id32"), -1.0)
+    for x in ("cc0", "cc1", "ca0", "ca1", "cb0", "cb1"):
+        cp(R(x, 2048, 4128, 2064), R("bl4", 4, 6))
+    cp(R("idf"), R("id32")); ts(R("nidf"), R("id32"), -1.0, A.mult)
+    tag[0] = "fk0"
+    iota(R("sel"), [[0, 2048]], 1, 0)
+    asel(R("sel"), R("sel"), [[1, 16], [16, 8], [0, 16]], 0)
 
-    ts(R("nzi"), R("lsi"), 0xFFF00, A.bitwise_and)
-    ts(R("nz"), R("nzi"), 31.0, A.mult, C(0), A.add)
-    tt(R("nu"), R("nz"), R("lsi"), A.add)
-    mm([(R("p2", 0, 128), R("nu"), R("pls"), True, True)])
-    act(R("l0"), R("p2", 0, 128))
-    cp(R("n0"), R("fpi"))
-    ts(R("pxh"), R("pxi"), 0xFFF00, A.bitwise_and)
-    for k in range(2):
-        ts(R("p%d" % (5 + k), 0, 288), R("pxh", 288 * k, 288 * k + 288), 31.0, A.mult, C(1), A.add)
-        tt(R("pk", 288 * k, 288 * k + 288), R("p%d" % (5 + k), 0, 288), R("pxi", 288 * k, 288 * k + 288), A.add)
-    cp(R("omf"), R("omi"))
-    for v in range(NV):
-        tt(R("omx", 128 * v, 128 * v + 128), G(R("omf"), R("oc", 8 * v, 8 * v + 8)), R("dg", 0, 128), A.mult)
-    mm([(R("p7", 8 * v, 8 * v + 8), R("omx", 128 * v, 128 * v + 128), R("blk"), True, True) for v in range(NV)])
-    act(R("nb"), R("p7", 0, 32), 4096.0)
+    def turn(o, oc, src, sc, mat):
+        return [(R(o, oc, oc + 64, p=p), R(src, sc, sc + 64, p=p), R(mat, 0, 64, p=p) if SCRATCH[mat][1][1] == 64
+                 else R(mat, 64 * p, 64 * p + 64, p=p), True, True) for p in range(2)]
 
-    def sort16(lo, hi, split, dst):
-        for k in range(3):
-            o = "ma" if k != 1 else "mb"
-            if k == split:
-                for h, (on, oc) in enumerate((("p0", 448), (o, 64))):
-                    x, y = R(lo[0], lo[1] + 32 * h, lo[1] + 32 * h + 32), R(hi[0], hi[1] + 32 * h, hi[1] + 32 * h + 32)
-                    tt(R(on, oc, oc + 64, 2), x, y, A.min); tt(R(on, oc + 1, oc + 64, 2), x, y, A.max)
-                lo, hi = ("p0", 448), (o, 64)
-            else:
-                x, y = R(lo[0], lo[1], lo[1] + 64), R(hi[0], hi[1], hi[1] + 64)
-                tt(R(o, 0, 128, 2), x, y, A.min); tt(R(o, 1, 128, 2), x, y, A.max)
-                lo, hi = (o, 0), (o, 64)
-        for h in range(2):
-            tt(R(dst, h, 128, 4), R("ma", 32 * h, 32 * h + 32), R("ma", 64 + 32 * h, 96 + 32 * h), A.min)
-            tt(R(dst, 2 + h, 128, 4), R("ma", 32 * h, 32 * h + 32), R("ma", 64 + 32 * h, 96 + 32 * h), A.max)
+    def records(dst, src, c):
+        ts(R("ea", c, c + 64), R(src, c, c + 64), 0xFFF00, A.bitwise_and)
+        ts(R("ec", c, c + 64), R("ea", c, c + 64), 2.0, A.mult, 400.0, A.add)
+        tt(R(dst, c, c + 64), R("ec", c, c + 64), R(src, c, c + 64), A.subtract)
 
-    def front(v):
-        b = str(v & 1)
-        gather(SIDE[0] if v else "v", R("pe"), G(R("pk"), R("n%d" % v)))
-        mm([(R("p4", 0, 128), R("pe"), R("ppx"), True, True)])
-        for q in range(4):
-            tt(R("mm", 2 * q, 256, 8), R("l%d" % v, 32 * q, 32 * q + 32), R("p4", 32 * q, 32 * q + 32), A.min)
-            tt(R("mm", 2 * q + 1, 256, 8), R("l%d" % v, 32 * q, 32 * q + 32), R("p4", 32 * q, 32 * q + 32), A.max)
-        lo, hi = ("mm", 0), ("mm", 128)
-        for k in range(3):
-            olo, ohi = ("p0", 128 * (k & 1)), ("ma" if k & 1 else "mb", 0)
-            for h, o in ((0, olo), (1, ohi)):
-                x, y = R(lo[0], lo[1] + 64 * h, lo[1] + 64 * h + 64), R(hi[0], hi[1] + 64 * h, hi[1] + 64 * h + 64)
-                tt(R(o[0], o[1], o[1] + 128, 2), x, y, A.min)
-                tt(R(o[0], o[1] + 1, o[1] + 128, 2), x, y, A.max)
-            lo, hi = olo, ohi
-        x, y = R(lo[0], lo[1], lo[1] + 128), R(hi[0], hi[1], hi[1] + 128)
-        tt(R("ki", 0, 256, 2), x, y, A.min); tt(R("ki", 1, 256, 2), x, y, A.max)
-        ts(R("xi"), R("ki"), 0x10FF, A.bitwise_and)
-        ts(R("zs"), R("ki"), 13, A.arith_shift_right)
-        cp(R("xf"), R("xi"))
-        un(SIDE[3], R("yf"), R("xf"), -2.0, 8192.0)
-        if v < NV - 1 and SIDE[4] == "s":
-            ts(R("p0", 256, 512), R("zs"), -1.0, A.mult)
-            tt(R("zc"), R("p0", 256, 512), R("cz"), A.add)
-            act(R("slb"), R("zc"), -1.0 / 256, 136 - 127.5 / 256 + (2047 + 255.0 / 256) / 256)
+    def listkeys(u, dst, c):
+        ts(R("hl", c, c + 64), R(u, 0, 64), R256 - 128 * UN, A.add, R256, A.subtract)
+        tt(R(u, 0, 60), R(u, 0, 60), R("hl", c + 4, c + 64), A.min)
+        tt(R(dst, c, c + 64), R(u, 0, 64), R("hl", c, c + 64), A.add)
+
+    def tables():
+        ts(R("tn"), R("pxi"), 257.0, A.add)
+        act(R("pxh"), R("tn"), 1.0, 2.0 ** 31 - 128)
+        act(R("pxh"), R("pxh"), 1.0, -2.0 ** 31)
+        for k in range(2):
+            a = 288 * k
+            mm(grp(R("p%d" % (5 + k), 0, 288), [(R("idz"), R("tn", a, a + 288)), (R("id32"), R("pxh", a, a + 288))]))
+            act(R("tn", a, a + 288), R("p%d" % (5 + k), 0, 288), 2.0, 145.0)
+
+    def bounds():
+        cp(R("omf"), R("omi"))
+        for k in range(4):
+            act(R("omx", k, 128, 4), R("omf"), R("bl4", k, k + 1))
+        mm(grp(R("p7", 0, 128), [(R("dg", 16, 144), R("omx"))]))
+        act(R("omy"), R("p7", 0, 128))
+        act(R("nb"), G(R("omy"), R("oc", 16, 18)), -1.0, 1.0)
+
+    def pixels(v, H):
+        c, w = 64 * H, "p%d" % (3 + H)
+        if v == 0:
+            cp(R("n0", 8 * H, 8 * H + 4), R("fpi", 4 * H, 4 * H + 4))
+            cp(R("pg", c, c + 64), G(R("pxi"), R("n0", 8 * H, 8 * H + 4)))
+            records("pe", "pg", c)
         else:
-            if v < NV - 1:
-                ts(R("p0", 256, 512), R("zs"), -1.0, A.mult)
-                tt(R("zc"), R("p0", 256, 512), R("cz"), A.add)
-            ts(R("slb"), R("zs"), 1.0 / 256, A.mult, 136 - 127.5 / 256, A.add)
-        scan(R("af"), R("yf"), R("xf"), 0.0, A.max, A.min)
-        scan(R("bf"), R("yf"), R("xf"), 4096.0, A.min, A.max)
-        for t, (src, bank) in enumerate((("af", "p2"), ("bf", "p3"))):
-            mm([(R(bank, 128 * h, 128 * h + 128), R(nm, h, 256, 2), R(idn), st, not st)
-                for h in range(2) for nm, idn, st in (("slb", "idb", True), (src, "id16", False))])
-            o = ("oa", "ob")[t] + b
-            ts(R(o, 0, 128), R(bank, 0, 128), C(5 + t), A.add, C(7), A.max)
-            ts(R(o, 128, 256), R(bank, 128, 256), -128.0 - 65536.0 * t, A.add, 0.0, A.max)
+            act(R("pe", c, c + 64), G(R("tn"), R("n%d" % v, 8 * H, 8 * H + 4)))
+        mm(turn(w, 128, "pe", c, "ppx"))
+        ts(R("hp", c, c + 64), R(w, 128, 192), R256 - 128 * UN, A.add, R256, A.subtract)
+        un(SIDE[4] if v else "v", R("hb", c, c + 64), R("hp", c, c + 64), 1.0, -200 * UN)
+        tt(R(w, 132, 192), R(w, 132, 192), R("hp", c, c + 60), A.min)
+        tt(R(w, 128, 192), R(w, 128, 192), R("hb", c, c + 64), A.add)
+
+    def front(v, H):
+        b, u, w, c = str(v & 1), "p%d" % (2 * H), "p%d" % (3 + H), 128 * H
+        last = v == NV - 1
+
+        def L(nme, a=0, e=128, st=1, p=None):
+            return R(nme, c + a, c + e, st, p)
+        x, y = R(w, 128, 192), R("l%d" % v, 64 * H, 64 * H + 64)
+        for o in ("ma", "mb", "ma"):
+            tt(L(o, 0, 128, 2), x, y, A.min); tt(L(o, 1, 128, 2), x, y, A.max)
+            x, y = L(o, 0, 64), L(o, 64, 128)
+        for h, (o, oc) in enumerate(((u, 128), ("mc", 64 * H))):
+            x, y = L("ma", 32 * h, 32 * h + 32), L("ma", 64 + 32 * h, 96 + 32 * h)
+            tt(R(o, oc, oc + 64, 2), x, y, A.min); tt(R(o, oc + 1, oc + 64, 2), x, y, A.max)
+        x, y = R(u, 128, 192), R("mc", 64 * H, 64 * H + 64)
+        tt(R(u, 0, 128, 2), x, y, A.min); tt(R(u, 1, 128, 2), x, y, A.max)
+        for g0, ng in parts("f"):
+            a, z = 32 * g0, 32 * (g0 + ng)
+            ts(L("hh", a, z), R(u, a, z), R512, A.add, R512, A.subtract)
+            tt(L("xf", a, z), R(u, a, z), L("hh", a, z), A.subtract)
+        un(SIDE[0], L("slb"), L("hh"), 8.0, 128 - 128.5 / 256)
+        ts(L("yf"), L("xf"), -8.0, A.mult, -200 * UN, A.add)
+        scan(L("bf"), L("yf"), L("xf"), -56 * UN, A.max, A.min)
+        scan(L("af"), L("yf"), L("xf"), 144 * UN, A.min, A.max)
+        for t, src, bank, oc, k in (("b", "bf", u, 256, -1024.0), ("a", "af", w, 0, 2176.0)):
+            mm([(R(bank, oc + 64 * h, oc + 64 * h + 64, p=p), L(nme, h, 128, 2, p), R(idn, 64 * p, 64 * p + 64, p=p), st, not st)
+                for h in range(2) for p in range(2) for nme, idn, st in (("slb", "idb", True), (src, "idm", False))])
+            o = "o" + t + b
+            ts(L(o, 0, 64), R(bank, oc, oc + 64), C(5 + (t == "b")), A.add, C(7), A.max)
+            ts(L(o, 64, 128), R(bank, oc + 64, oc + 128), k, A.add)
+        scan(L("ln", 0, 127), L("hh", 1, 128), L("hh", 0, 127), 0.0, A.max, A.subtract)
+        ts(L("ln", 31, 128, 32), L("hh", 31, 128, 32), -1.0, A.mult, 4097 * 512 * UN, A.add)
+        ss, e = "ss" + b, 2048 * H
+        how = SG[2 * v + H]
+        fused = how == "f"
         k = 0
         for h in range(2):
-            for hf in range(2):
-                for t in "ab":
-                    gather(SG[v][k], R("s" + t + b, 2048 * hf + h, 2048 * hf + 2048, 2),
-                           G(R("tsg"), R("o" + t + b, 128 * h + 64 * hf, 128 * h + 64 * hf + 64)))
-                    k += 1
-            mm([(R("p3", s, 512, 32), R("s" + t + b, s, 4096, 32),
-                 R("rh", 32, 48) if s == 0 else R("rh", 0, 16) if t == "a" else R("rh", 16, 32), t == "a", t == "b")
-                for s in range(h, 32, 2) for t in "ab"])
-        if v < NV - 1:
-            tt(R("ln", 0, 255), R("p0", 256, 511), R("zs", 1, 256), A.add)
-        else:
-            tt(R("ln", 0, 255), R("zs", 1, 256), R("zs", 0, 255), A.subtract)
-        ts(R("ln", 31, 256, 32), R("zs", 31, 256, 32), -1.0, A.mult, 2048.0, A.add)
-        ms(R("ln", 0, 256, 32), -1048576.0)
-        act(R("rst0", 0, 256, 32), R("nb", 8 * v, 8 * v + 8))
-        if v < NV - 1:
-            mm([(R("p2", 256, 512), R("idc"), R("oneb", 0, 256), True, False), (R("p2", 256, 512), R("idp"), R("bf"), False, False),
-                (R("p2", 256, 512), R("idn"), R("af"), False, True)])
-            mm([(R("p4", 256, 512), R("idc"), R("oneb", 0, 256), True, False), (R("p4", 256, 512), R("idb"), R("oneb", 256, 512), False, False),
-                (R("p4", 256, 512), R("idp"), R("bf"), False, False), (R("p4", 256, 512), R("idp"), R("af"), False, True)])
+            a = 0
+            for n in SQ[h]:
+                o = (e + 32 * a + h, e + 32 * (a + n), 2)
+                wa, wb = (G(R("tsg"), L(x + b, 64 * h + a, 64 * h + a + n)) for x in ("oa", "ob"))
+                if fused:
+                    act(R("sb", *o), wb); tt(R(ss, *o), wa, R("sb", *o), A.add)
+                else:
+                    gather(how[k % len(how)], R("sb", *o), wb); gather(how[(k + 1) % len(how)], R(ss, *o), wa)
+                a += n; k += 2
+            for s0 in (h, 16 + h):
+                lst = []
+                for s in range(s0, s0 + 16, 2):
+                    lst += grp(R(w, s, 512, 32, 0), [(R(ss, e + s, e + 2048, 32), R("rh", 0, 16) if s else R("rh", 16, 32))]
+                               + ([] if last and fused or s == 0 else [(R("sb", e + s, e + 2048, 32), R("rh", 16, 32) if fused else R("rh", 48, 64))])
+                               + ([(R("c1", 0, 64), R("rh", 32, 48))] if s == 31 else []))
+                mm(lst)
+        if not fused:
+            tag[0] = "fa" + tag[0][2]
+            x, y = R(ss, e, e + 2048), R("sb", e, e + 2048)
+            dma("g", x[0], y[0], [x, y], [x], 1 << 19, DA, accum_op=A.add)
+        tag[0] = "ww" + tag[0][2]
+        if not last:
+            act(L("ln", 0, 128, 32), R("ones", 0, 4))
+        act(R(u, 0, 128), L("ln"), -0.5, 1.0)
+        act(L("rst", 0, 128, 32), R("nb", 8 * v + 4 * H, 8 * v + 4 * H + 4))
+        if not last:
+            act(L("den"), L("ln"), -2048.0, 1.0, ACT.Relu)
+            act(L("zc"), L("hh"), -0.5, 1.0)
+            mm(grp(R(u, 256, 384), [(R("idb"), R("c100")), (R("idh"), L("af")), (R("nidh"), L("bf"))])
+               + grp(R(u, 384, 512), [(R("idb"), R("c44")), (R("idb"), L("den"))]
+                     + ([(R("nidh"), L("af")), (R("nidh"), L("bf"))] if SIDE[1] == "s" else [(R("nidb"), L("af"))])))
 
-    def seen(v):
-        b = str(v & 1)
-        tt(R("nw"), R("p3", 0, 256), R("ln"), A.mult)
-        scan(R("p0", 256, 512), R("nw"), R("rst0"), 0.0, A.add, A.max)
-        tt(R("lv", 1, 256), R("p0", 256, 511), R("ln", 1, 256), A.min)
-        mm([(R("p2", 128 * h, 128 * h + 128), R("lv", h, 256, 2), R("id32"), True, True) for h in range(2)])
-        tag[0] = "n%d" % v if OLN else "f%da" % v
-        ts(R("lh" + b, 0, 128), R("p2", 0, 128), C(8), A.max)
-        cp(R("lh" + b, 128, 256), R("p2", 128, 256))
-        tt(R("lh" + b, 256, 512), R("p2", 0, 256), R("lh" + b, 0, 256), A.subtract)
-        for hf in range(2):
-            x, y = R("sa" + b, 2048 * hf, 2048 * hf + 2048), R("sb" + b, 2048 * hf, 2048 * hf + 2048)
-            dma("g", x[0], y[0], [x, y], [x], 1 << 19, accum_op=A.add)
+    def seen(v, H):
+        u, w, c, d = "p%d" % (2 * H), "p%d" % (3 + H), 128 * H, 136 * H
+        for p in range(2):
+            tt(R("nw", c, c + 128, p=p), R(w, 128 * p, 128 * p + 128, p=0), R("ln", c, c + 128, p=p), A.mult)
+        if v < NV - 1:
+            for p in range(2):
+                if SIDE[1] == "s":
+                    act(R("tc", c, c + 128, p=p), R(w, 256 + 128 * p, 384 + 128 * p, p=0), 1.0, -0.5, ACT.Sign)
+                else:
+                    ts(R("tc", c, c + 128, p=p), R(w, 256 + 128 * p, 384 + 128 * p, p=0), 0.0, A.is_gt, 2.0, A.mult)
+        for g0, ng in parts("s"):
+            a, z = 32 * g0, 32 * (g0 + ng)
+            scan(R("rr", d + a + 1, d + z + 1), R("nw", c + a, c + z), R("rst", c + a, c + z), 1.0, A.add, A.min)
+            tt(R("lv", c + a, c + z), R(u, a, z), R("rr", d + a, d + z), A.max)
 
-    def remake(v):
-        if SIDE[5] == "s":
-            act(R("tc"), R("p3", 256, 512), 1.0, -0.5, ACT.Sign)
-        else:
-            ts(R("e1"), R("p3", 256, 512), 0.0, A.is_gt, 2.0, A.mult)
-            ts(R("tc"), R("e1"), -1.0, A.add)
-        tt(R("nm"), R("p2", 256, 512), R("tc"), A.mult)
-        tt(R("p0", 0, 256), R("p4", 256, 512), R("nm"), A.add)
-        if SIDE[6] == "s":
-            act(R("den"), R("lv"), -8192.0, 8192.0, ACT.Relu)
-        else:
-            ts(R("den"), R("lv"), 0.0, A.is_le, 8192.0, A.mult)
-        tt(R("xa"), R("p0", 0, 256), R("den"), A.subtract)
-        tt(R("p0", 256, 512), R("zc"), R("p0", 0, 256), A.subtract)
-        scan(R("ff", 1, 257), R("den"), R("xa"), 0.9, A.min, A.max)
-        tt(R("xb"), R("p0", 256, 512), R("den"), A.add)
-        scan(R("zz"), R("rstb"), R("xb"), 0.0, A.max, A.min)
-        tag[0] = "n%d" % v
-        ts(R("n8"), R("ff", 32, 257, 32), 1024.0, A.mult)
-        tt(R("t8"), R("zz", 31, 256, 32), R("ff", 32, 257, 32), A.add)
-        ts(R("q8"), R("t8"), -1.0 / 1024, A.mult, (4095 + 255.0 / 256 - 511.5) / 1024, A.add)
-        tt(R("nam"), R("n8"), R("q8"), A.add)
-        tt(R("nx"), G(R("nam"), R("oc", 32, 41)), R("dg", 0, 144), A.mult)
-        mm([(R("p3", 0, 8), R("nx", 16, 144), R("blk"), True, True), (R("p3", 8, 16), R("nx", 0, 128), R("blk"), True, True)])
-        ts(R("nown"), R("p3", 0, 8), C(9), A.add)
-        ts(R("m%d" % v), R("p3", 8, 16), C(10), A.add)
-        send(R("m%d" % v), R("n%d" % (v + 1)), "rn%d" % v, 2048)
-        if SIDE[1] == "v":
-            ts(R("te"), G(R("pk"), R("nown")), -4352.0, A.add)
-        else:
-            act(R("te"), G(R("pk"), R("nown")), 1.0, -4352.0)
-        mm([(R("p4", 128, 256), R("te"), R("ptl"), True, True)])
-        tag[0] = "r%d" % v
-        un(SIDE[2], R("thr"), R("t8"), -8192.0, 16785376.0)
-        gather(SIDE[2], R("thb"), G(R("thr"), R("oc", 48, 56)))
-        tt(R("p0", 0, 256), R("ff", 1, 257), R("ff", 0, 256), A.is_equal)
-        ts(R("nm"), R("p0", 0, 256), -M1, A.mult, M1, A.add)
-        tt(R("tc"), R("p0", 0, 256), R("sc"), A.mult)
-        tt(R("vh"), R("p0", 256, 512), R("nm"), A.min)
-        scan(R("p0", 0, 256), R("rstm"), R("nm"), 0.0, A.min, A.add)
-        tt(R("ei"), R("p0", 0, 256), R("tc"), A.add)
-        ts(R("e1"), R("ei"), 0x8888, A.bitwise_and)
-        ts(R("e2"), R("e1"), M2, A.mult)
-        ts(R("e3"), R("e2"), 0xF000, A.bitwise_and)
-        tt(R("p0", 0, 128), R("e3", 0, 256, 2), R("vh", 0, 256, 2), A.add)
-        tt(R("ta"), R("e3", 1, 256, 2), R("vh", 1, 256, 2), A.add)
-        e, o = 0, "ta"
-        for k in range(4):
-            e2, o2 = 128 - e, ("tb" if o == "ta" else "ta")
+    def remake(v, H):
+        u, w, c, d, e, k = "p%d" % (2 * H), "p%d" % (3 + H), 128 * H, 136 * H, 192 * H, 64 * H
+        nm, un_ = "nm%d" % (v & 1), tag[0][1:]
+
+        def L(nme, a=0, z=128, st=1):
+            return R(nme, c + a, c + z, st)
+
+        def S(nme):
+            return R(nme, 4 * H, 4 * H + 4)
+
+        def J(nme, a=0, st=1):
+            return R(nme, e + a, e + 192, st)
+        for g0, ng in parts("n"):
+            a, z = 32 * g0, 32 * (g0 + ng)
+            tt(L("nm", a, z), R(u, 256 + a, 256 + z), L("tc", a, z), A.mult)
+            tt(R(u, a, z), R(u, 384 + a, 384 + z), L("nm", a, z), A.add)
+            tt(R(u, 128 + a, 128 + z), R(u, a, z), L("zc", a, z), A.add)
+            scan(L("zz", a, z, -1), R(u, 128 + a, 128 + z, -1), R("rr", d + a, d + z, -1), 1.0, A.min, A.max)
+        tag[0] = "n" + un_
+        ts(S("e8"), L("zz", 1, 128, 32), 4.0 / UN, A.mult)
+        ts(S("n8"), S("e8"), 1023, A.bitwise_and)
+        ts(S("q8"), S("e8"), 20, A.arith_shift_right)
+        tt(R("nam", 8 * H, 8 * H + 4), S("n8"), S("q8"), A.subtract)
+        tt(R("nx", 144 * H, 144 * H + 144), G(R("nam", 8 * H, 8 * H + 4), R("oc", 4, 13)), R("dg"), A.mult)
+        mm([(R(w, 0, 8), R("nx", 144 * H + 16, 144 * H + 144), R("bl4"), True, True),
+            (R(w, 8, 16), R("nx", 144 * H, 144 * H + 128), R("bl4"), True, True)])
+        ts(R(nm, 16 * H, 16 * H + 16), R(w, 0, 16), 3.0, A.add)
+        send(R(nm, 16 * H + 8, 16 * H + 12), R("n%d" % (v + 1), 8 * H, 8 * H + 4), "rn%d" % (2 * v + H), RN)
+        un(SIDE[2], R("te", k, k + 64), G(R("tn"), R(nm, 16 * H, 16 * H + 4)), -UN, 1 + 144 * UN)
+        mm(turn(w, 64, "te", k, "id32"))
+        tt(R("t8", 8 * H, 8 * H + 4), S("e8"), S("n8"), A.subtract)
+        un(SIDE[3], R("thb", k, k + 64), G(R("t8", 8 * H, 8 * H + 4), R("oc", 0, 4)), UN / 4, 0.0)
+        tag[0] = "r" + un_
+        for g0, ng in parts("r"):
+            a, z = 32 * g0, 32 * (g0 + ng)
+            scan(R("ff", d + a + 1, d + z + 1), L("ln", a, z), R(u, a, z), 500 * UN, A.max, A.min)
+            tt(R(u, a, z), R(u, a, z), R("ff", d + a, d + z), A.not_equal)
+            tt(R3("live", 4 * H + g0, 0, 32, 1, ng), R(u, a, z), L("lv", a, z), A.is_gt)
+            tt(R3("p1", g0, 0, 32, 1, ng), R(u, 128 + a, 128 + z), R3("live", 4 * H + g0, 0, 32, 1, ng), A.min)
+        tt(R3("live", 4 * H, 32, 48), R(w, 64, 128), R("thb", k, k + 64), A.is_lt)
+        tt(R3("p1", 0, 32, 48), R(w, 64, 128), R3("live", 4 * H, 32, 48), A.min)
+        for g0, ng in parts("j"):
+            a, z = 48 * g0, 48 * (g0 + ng)
+            n2m, tq, ei, e1, e2 = (R(x, e + a, e + z) for x in ("n2m", "tq", "ei", "e1", "e2"))
+            un(SIDE[5], n2m, R3("live", 4 * H + g0, 0, 48, 1, ng), M1, -M1)
+            tt(tq, R3("p1", 4 + g0, 0, 48, 1, ng), R3("live", 4 * H + g0, 0, 48, 1, ng), A.mult)
+            scan(R(u, a, z), R("rstm", a, z), n2m, 0.0, A.max, A.add)
+            tt(ei, R(u, a, z), tq, A.add)
+            ts(e1, ei, MASK, A.bitwise_and)
+            ts(e2, e1, M2, A.mult)
+            ts(e1, e2, 15, A.bitwise_and)
+        f = 96 * H
+        tt(R(u, 0, 96), R3("p1", 0, 0, 48, 2), J("e1", 0, 2), A.add)
+        tt(R("ta", f, f + 96), R3("p1", 0, 1, 48, 2), J("e1", 1, 2), A.add)
+        a, o = 0, "ta"
+        for st in range(3):
+            a2, o2 = 96 - a, ("tb" if o == "ta" else "ta")
             for h in range(2):
-                x, y = R("p0", e + h, e + 128, 2), R(o, h, 128, 2)
-                for j, op in enumerate((A.max, A.min)):
-                    tt(R("p0", e2 + 64 * j, e2 + 64 * j + 64) if h == 0 else R(o2, 64 * j, 64 * j + 64), x, y, op)
-            e, o = e2, o2
-        tt(R("p0", 128, 256), R("p0", e, e + 128), R(o), A.max)
-        tt(R("nu"), R("posc"), R("p0", 128, 256), A.subtract)
-        ts(R("nzi"), R("nu"), 111.0 / 256 - 0.7, A.add)
-        ts(R("p0", 0, 128), R("nu"), 256.0, A.mult, -1.0, A.add)
-        ts(R("nz"), R("nzi"), 7936.0, A.mult, -TWO24, A.add)
-        tt(R("nkk"), R("p0", 0, 128), R("nz"), A.add)
-        tt(R("tm"), R("p4", 128, 256), R("thb"), A.is_lt)
-        un(SIDE[7], R("nw1"), R("tm"), KF + TWO24, -TWO24)
-        tt(R("p0", 384, 448), R("p4", 128, 192), R("nw1", 0, 64), A.max)
-        tt(R("nk", 64, 128), R("p4", 192, 256), R("nw1", 64, 128), A.max)
-        sort16(("p0", 384), ("nk", 64), 1, "tm")
-        for q in range(4):
-            tt(R("uu", q, 128, 4), R("tm", 32 * q, 32 * q + 32), R("nkk", q, 128, 4), A.min)
-        sort16(("uu", 0), ("uu", 64), 0, "o%d" % v)
-        send(R("o%d" % v), R("l%d" % (v + 1)), "rl%d" % v, 65536)
+                x, y = R(u, a + h, a + 96, 2), R(o, f + h, f + 96, 2)
+                for j, op in enumerate((A.min, A.max)):
+                    tt(R(u, a2 + 48 * j, a2 + 48 * j + 48) if h == 0 else R(o2, f + 48 * j, f + 48 * j + 48), x, y, op)
+            a, o = a2, o2
+        for j, op in enumerate((A.min, A.max)):
+            tt(R("yy", e + 96 * j, e + 96 * j + 96), R(u, a, a + 96), R(o, f, f + 96), op)
+        tt(R(u, 192, 256), J("yy", 0, 3), J("yy", 1, 3), A.max)
+        tt(R(u, 192, 256), R(u, 192, 256), J("yy", 2, 3), A.max)
+        tt(R(u, 0, 64), R("posc"), R(u, 192, 256), A.subtract)
+        listkeys(u, "o%d" % (v & 1), k)
+        send(R("o%d" % (v & 1), k, k + 64), R("l%d" % (v + 1), k, k + 64), "rl%d" % (2 * v + H), RL)
 
-    def floats(v):
-        b = str(v & 1)
-        al = "al" + b
-        tag[0] = "f%dc" % v
-        n = 128 // CQ
+    def floats(v, H):
+        b, n, c, e = str(v & 1), 2 * v + H, 128 * H, 2048 * H
+        al, lh, z = "al" + b, "lh" + b, 2064 * H
+        tag[0] = "fa%d" % n
+        bank = "p" + BANKL[n]
+        lst = []
+        for h in range(2):
+            o = 64 * h
+            lst += [(R(bank, o, o + 64), R("ct", 128 * h, 128 * h + 128), R("idb", 0, 64), True, False)]
+            lst += [(R(bank, o, o + 64, p=p), R("lv", c + h, c + 128, 2, p), R("idl", 64 * p, 64 * p + 64, p=p), False, True) for p in range(2)]
+        mm(lst)
+        act(R(lh, 2 * c, 2 * c + 128), R(bank, 0, 128))
+        tt(R(lh, 2 * c + 128, 2 * c + 256), R(bank, 0, 128), R(lh, 2 * c, 2 * c + 128), A.subtract)
+        tag[0] = "fc%d" % n
+        m = 64 // CQ
+        joint = CM[n] == "f"
+        cols = [("cc" + b, "idf", "nidf")] if joint else [("ca" + b, "idb", "nidb"), ("cb" + b, "idb", "nidb")]
         for q in range(CQ):
             for h in range(2):
-                for t in "ab":
-                    gather(CO[v][4 * (2 * q // CQ) + 2 * h + (t == "b")], R("c" + t + b, 32 * n * q + h, 32 * n * (q + 1), 2),
-                           G(R("tco"), R("o" + t + b, 128 * h + n * q, 128 * h + n * (q + 1))))
-        tag[0] = "f%da" % v
-        n = 128 // AH[v]
-        k = 0
-        for q in range(AH[v]):
-            for s0 in range(0, 32, 512 // n):
-                bank = "p" + BANKA[v][k]; k += 1
-                lst = []
-                for j in range(512 // n):
-                    h, r = (s0 + j) >> 4, (s0 + j) & 15
-                    for part in range(1 if s0 + j == 0 else 2):
-                        a = 256 * part + 128 * h + n * q
-                        lst.append((R(bank, n * j, n * j + n), R("sel", 128 * r, 128 * r + 128), R("lh" + b, a, a + n),
-                                    part == 0, part == 1 or s0 + j == 0))
-                mm(lst)
-                for j in range(512 // n):
-                    h, r = (s0 + j) >> 4, (s0 + j) & 15
-                    tt(R(al, 2048 * h + 16 * n * q + r, 2048 * h + 16 * n * (q + 1), 16), R(bank, n * j, n * j + n),
-                       R("sa" + b, 32 * n * q + 2 * r + h, 32 * n * (q + 1), 32), A.mult)
-        tag[0] = "f%do" % v
-        for c in range(8):
-            q, h = c >> 1, c & 1
-            un(OM[v][c], R("om" + b, 1024 * q + h, 1024 * q + 1024, 2), R(al, 2048 * h + 512 * q, 2048 * h + 512 * q + 512), -2.0 ** -17, 1.0)
-        tag[0] = "f%du" % v
-        for c in range(8):
-            bank = "p" + BANKS[v][c]; a = 512 * c
-            mm([(R(bank), R("idb"), R("ca" + b, a + 1, a + 513), True, False), (R(bank), R("idb"), R("cb" + b, a + 1, a + 513), False, False),
-                (R(bank), R("nidb"), R("ca" + b, a, a + 512), False, False), (R(bank), R("nidb"), R("cb" + b, a, a + 512), False, True)])
-            scan(R("ub", a, a + 512, -1), R(bank, 0, 512, -1), R("om" + b, a, a + 512, -1), 0.0, A.add, A.mult)
-        tag[0] = "f%dy" % v
-        for hf in range(2):
-            a = 1024 * hf
-            ns = 32
-            if FOLD[v][hf] == "d":
-                ns = 16
-                x, y = R(al, a, a + 1024), R(al, 2048 + a, 3072 + a)
-                dma("g", x[0], y[0], [x, y], [x], 1 << 19, accum_op=A.add)
-            for s0 in range(0, ns, 4):
-                mm([(R("p7", 128 + 64 * hf, 192 + 64 * hf), R("id32"), R(al, 2048 * (s >> 4) + a + (s & 15), 2048 * (s >> 4) + a + 1024, 16),
-                     s == 0, s == ns - 1) for s in range(s0, s0 + 4)])
-        mm([(R("p7", 0, 128), R("idb"), R("ca" + b, 1, 4096, 32), True, False), (R("p7", 0, 128), R("idb"), R("cb" + b, 1, 4096, 32), False, False),
-            (R("p7", 0, 128), R("id32"), R("ub", 1, 4096, 32), False, True)])
-        act(R("yo" + b, 128, 256), R("p7", 128, 256), 2.0 ** -14, -8.0)
-        act(R("yo" + b, 0, 128), R("p7", 0, 128))
-        dma("y", T.yt[:, 128 * v:128 * v + 128], R("yo" + b, 128, 256)[0], [R("yo" + b, 128, 256)], [], 65536)
-        dma("y", T.yc[:, 128 * v:128 * v + 128], R("yo" + b, 0, 128)[0], [R("yo" + b, 0, 128)], [], 65536)
+                a, x = 32 * m * q + h, 32 * m * (q + 1)
+                wa, wb = (G(R("tco"), R(o + b, c + 64 * h + m * q, c + 64 * h + m * (q + 1))) for o in ("oa", "ob"))
+                gather(CO[n][(2 * q + h) % 4], R("cb" + b, z + a, z + x, 2), wb)
+                if joint:
+                    tt(R("cc" + b, z + a, z + x, 2), wa, R("cb" + b, z + a, z + x, 2), A.add)
+                else:
+                    gather(CO[n][4 + (2 * q + h) % 4], R("ca" + b, z + a, z + x, 2), wa)
+        tag[0] = "fa%d" % n
+        nb = 8 if FOLD[n] == "3" else 4
+        bs, nj = 2048 // nb, 32 // nb
+        for q in range(4):
+            bank = "p" + BANKA[n][q % len(BANKA[n])]
+            part = [(i // nj, i % nj) for i in range(8 * q, 8 * q + 8)]
+            lst = []
+            for i, (k, j) in enumerate(part):
+                h, r = k & 1, (nb * j + k) >> 1
+                lst += grp(R(bank, 64 * i, 64 * i + 64), [(R("sel", 128 * r, 128 * r + 128), R(lh, 2 * c + 128 * x + 64 * h, 2 * c + 128 * x + 64 * h + 64))
+                                                         for x in range(1 if j + k == 0 else 2)])
+            mm(lst)
+            for i, (k, j) in enumerate(part):
+                tt(R(al, e + bs * k + j, e + bs * k + bs, nj), R(bank, 64 * i, 64 * i + 64), R("ss" + b, e + nb * j + k, e + 2048, 32), A.mult)
+        tag[0] = "fo%d" % n
+        for k in range(nb):
+            un(OM[n][k % 4], R("om" + b, e + k, e + 2048, nb), R(al, e + bs * k, e + bs * k + bs), -2.0 ** -17, 1.0)
+        tag[0] = "fu%d" % n
+        for k in range(4):
+            bank = "p" + BANKS[n][k % len(BANKS[n])]; a = z + 512 * k
+            mm(grp(R(bank), [(R(p), R(x, a + 1, a + 513)) for x, p, q in cols] + [(R(q), R(x, a, a + 512)) for x, p, q in cols]))
+            a = e + 512 * k
+            for x in range(0, 512, UQ):
+                scan(R("ub", a + x, a + x + UQ, -1), R(bank, x, x + UQ, -1), R("om" + b, a + x, a + x + UQ, -1), 0.0, A.add, A.mult)
+        tag[0] = "fy%d" % n
+        ns = 32
+        pt, pc = "p" + BANKO[n][0], "p" + BANKO[n][1]
+        for k in range(int(FOLD[n])):
+            ns //= 2
+            x, y = R(al, e, e + 64 * ns), R(al, e + 64 * ns, e + 128 * ns)
+            dma("g", x[0], y[0], [x, y], [x], 32768 * ns, DF if v < NV - 1 else DA, accum_op=A.add)
+        for s0 in range(0, ns, 4):
+            mm([(R(pt, 64, 128), R("id32"), R(al, e + bs * (s // nj) + s % nj, e + bs * (s // nj) + bs, nj), s == 0, s == ns - 1)
+                for s in range(s0, s0 + 4)])
+        act(R("yo" + b, c + 64, c + 128), R(pt, 64, 128), 2.0 ** -14, -8.0)
+        mm(grp(R(pc, 0, 64), [(R(p), R(x, z + 1, z + 2048, 32)) for x, p, q in cols] + [(R("id32"), R("ub", e + 1, e + 2048, 32))]))
+        act(R("yo" + b, c, c + 64), R(pc, 0, 64))
+        for y, a in ((T.yt, c + 64), (T.yc, c)):
+            dma("y", y[:, 64 * n:64 * n + 64], R("yo" + b, a, a + 64)[0], [R("yo" + b, a, a + 64)], [], 32768)
 
-    for v in range(NV):
-        tag[0] = "m%d" % v
-        front(v)
-        tag[0] = "s%d" % v
-        seen(v)
+    for H in range(2):
+        tag[0] = "mm%d" % H
+        records("eb", "lsi", 64 * H)
+        mm(turn("p%d" % (2 * H), 0, "eb", 64 * H, "pls"))
+        listkeys("p%d" % (2 * H), "l0", 64 * H)
+        pixels(0, H)
+    tag[0] = "ww0"
+    bounds(); tables()
+    for n in range(2 * NV):
+        v, H = n >> 1, n & 1
+        tag[0] = "mm%d" % n
+        front(v, H)
+        tag[0] = "ss%d" % n
+        seen(v, H)
         if v < NV - 1:
-            tag[0] = "r%d" % v
-            remake(v)
-        floats(v)
+            tag[0] = "rr%d" % n
+            remake(v, H)
+            tag[0] = "mm%d" % (n + 2)
+            pixels(v + 1, H)
+        floats(v, H)
 
     n = len(ops)
     before = [sorted(o["d"] | o["o"]) for o in ops]
@@ -521,77 +587,60 @@ def rank_program(g, core, T, topo):
         for d in before[i]:
             after[d].append(i)
 
-    def sched(pr):
-        left = [len(x) for x in before]
-        rdy = [0.0] * n
+    lag = [{d: (ops[d]["l"] + XLAT if ops[d]["e"] != o["e"] or ops[d]["sem"] else ops[d]["l"] + LAT if d in o["d"] else 0.0)
+            for d in o["d"] | o["o"]} for o in ops]
+
+    def sched(key, back):
+        pre, post = (after, before) if back else (before, after)
+        left = [len(x) for x in pre]
+        rdy = [ops[i]["l"] if back else 0.0 for i in range(n)]
         free = {e: 0.0 for e in "vspgyr"}
         cand = {e: [] for e in free}
-        sq = {e: [] for e in free}
-        gl = []; fin = [0.0] * n
+        at = [0.0] * n
         for i in range(n):
             if left[i] == 0:
                 cand[ops[i]["e"]].append(i)
-        done = set()
-        nxc = {e: [i for i in range(n) if ops[i]["e"] == e and ops[i]["t"][0] in "msrn"] for e in free}
-        while len(done) < n:
+        for step in range(n):
             best = None
             for e in cand:
-                if not cand[e]:
-                    continue
-                t0 = max(free[e], min(rdy[i] for i in cand[e]))
-                i = max((i for i in cand[e] if rdy[i] <= t0), key=lambda j: pr[j])
-                soon = [j for j in cand[e] if rdy[j] <= t0 + LOOK * ops[i]["c"] and pr[j] > pr[i] + 3000 and ops[i]["c"] > 300]
-                if soon:
-                    i = min(soon, key=lambda j: rdy[j])
-                t = max(free[e], rdy[i])
-                if best is None or t < best[0]:
-                    best = (t, e, i)
+                if cand[e]:
+                    t = max(free[e], min(rdy[i] for i in cand[e]))
+                    i = min((i for i in cand[e] if rdy[i] <= t), key=lambda j: key[j])
+                    soon = [j for j in cand[e] if t < rdy[j] <= t + HOLD[e] * ops[i]["c"] and key[j] < key[i] - AHEAD]
+                    if soon:
+                        x = min(rdy[j] for j in soon)
+                        fit = [j for j in cand[e] if rdy[j] <= t and ops[j]["c"] <= x - t + 40]
+                        i = min(fit, key=lambda j: key[j]) if fit else min(soon, key=lambda j: rdy[j])
+                    t = max(t, rdy[i])
+                    if best is None or t < best[0]:
+                        best = (t, e, i)
             t, e, i = best
-            if ops[i]["t"][0] == "f" and ops[i]["c"] > 300:
-                memo = {}
-
-                def est(j, depth):
-                    if j not in memo:
-                        x = max(rdy[j], t)
-                        if left[j]:
-                            x = 1e18 if depth == 0 else max([x] + [est(d, depth - 1) + ops[d]["c"] + ops[d]["l"] + LAT for d in before[j] if d not in done])
-                        memo[j] = max(x, free[ops[j]["e"]]) if ops[j]["e"] != e else x
-                    return memo[j]
-                while nxc[e] and nxc[e][0] in done:
-                    nxc[e].pop(0)
-                x = min([est(j, 8) for j in nxc[e][:4] if j not in done] + [1e18])
-                if t < x < t + HOLD[e] * ops[i]["c"]:
-                    fit = [j for j in cand[e] if rdy[j] <= t and ops[j]["c"] <= x - t + 60]
-                    if fit:
-                        i = max(fit, key=lambda j: pr[j])
-                    else:
-                        free[e] = x
-                        continue
-            done.add(i)
-            cand[e].remove(i); sq[e].append(i); gl.append(i)
+            cand[e].remove(i); at[i] = t
             free[e] = t + ops[i]["c"]
-            fin[i] = free[e] + ops[i]["l"]
-            for j in after[i]:
-                if i in ops[j]["d"] or e != ops[j]["e"]:
-                    rdy[j] = max(rdy[j], fin[i] + LAT)
+            for j in post[i]:
+                rdy[j] = max(rdy[j], free[e] + (lag[i][j] if back else lag[j][i]))
                 left[j] -= 1
                 if left[j] == 0:
                     cand[ops[j]["e"]].append(j)
-        return max(fin), sq, gl, fin
+        return at
 
     if "plan" not in PLAN:
         pr = [0.0] * n
         for i in range(n - 1, -1, -1):
-            pr[i] = ops[i]["c"] + ops[i]["l"] + max([pr[j] + LAT for j in after[i]] + [0.0])
-        for i, o in enumerate(ops):
-            t = o["t"]
-            if t[0] == "f":
-                pr[i] = 1e6 + 1000.0 * URG[t[2]][int(t[1])] - i
-            elif t[0] == "n":
-                pr[i] += 2e6
-            else:
-                pr[i] += 1e6 + (1e6 if t == "k" and o["e"] != "g" and o["c"] < 100 else 0.0)
-        PLAN["plan"] = sched(pr)
+            pr[i] = ops[i]["c"] + max([pr[j] + lag[j][i] for j in after[i]] + [ops[i]["l"]])
+        key = [-pr[i] - (1000.0 * URG[o["t"][1]] if o["t"][0] == "f" else 0.0 if o["t"] == "k" or int(o["t"][2]) & 1 else 1000.0 * STAG)
+               for i, o in enumerate(ops)]
+        best = None
+        for k in range(PASSES):
+            at = sched(key, False)
+            end = max(at[i] + ops[i]["c"] + ops[i]["l"] for i in range(n))
+            if best is None or end < best[0]:
+                best = (end, at)
+            bt = sched([-at[i] - ops[i]["c"] for i in range(n)], True)
+            key = [-bt[i] - ops[i]["c"] for i in range(n)]
+        at = best[1]
+        gl = sorted(range(n), key=lambda i: (at[i], i))
+        PLAN["plan"] = (best[0], {e: [i for i in gl if ops[i]["e"] == e] for e in "vspgyr"}, gl, [at[i] + ops[i]["c"] + ops[i]["l"] for i in range(n)])
     PLAN["ops"] = ops
     seq, glob = PLAN["plan"][1:3]
     gpos = {i: k for k, i in enumerate(glob)}

import numpy as np
from concourse.mybir import AluOpType, ActivationFunctionType

F, B, I, U = "float32", "bfloat16", "int32", "uint16"
NV = 4
WT = 2320
SCRATCH = {}


def _s(names, n, d):
    for x in names.split():
        SCRATCH[x] = ("sbuf", [128, n], d)


_s("tsg tco", WT, B)
_s("pxi", 576, I); _s("tn pxh", 576, F); _s("lsi pg ea ec", 128, I)
_s("fpi", 8, I); _s("omi", 32, I); _s("omf nb", 32, F); _s("omx omy", 128, F)
_s("sel", 2048, B)
_s("ones id32 idl idz", 128, F); _s("ppx pls posc", 64, F); _s("idb nidb idh nidh idm", 128, B)
_s("dgi", 144, I); _s("dg", 144, F); _s("blk bl4", 8, F); _s("rh", 64, B)
_s("pid", 8, I); _s("col", 16, F); _s("oci", 32, I); _s("oc", 32, U)
_s("rst", 256, F); _s("rstm", 192, F); _s("c44 c100", 128, B); _s("c1", 64, B); _s("ct", 256, B)
_s("l0 l1 l2 l3 o0 o1", 128, F); _s("n0 n1 n2 n3", 16, U); _s("nm0 nm1", 32, U)
_s("eb pe te hp hb hl mc thb", 128, F)
_s("ma mb hh ln nw lv tc nm zz zc", 256, F); _s("rr ff", 272, F); _s("xf yf af bf slb den", 256, B)
_s("n2m tq yy", 384, F); _s("ei e1 e2", 384, I); _s("ta tb", 192, F)
SCRATCH["live"] = ("sbuf", [128, 8, 48], F)
_s("oa0 oa1 ob0 ob1", 256, U); _s("lh0 lh1", 512, B)
_s("nam t8", 16, F); _s("q8 e8 n8", 8, I); _s("nx", 288, F)
_s("sb ss0 ss1", 4096, B); _s("ca0 ca1 cb0 cb1", 4128, B); _s("cc0 cc1", 4128, "float16"); _s("idf nidf", 128, "float16")
_s("al0 al1 ub om0 om1", 4096, F); _s("yo0 yo1", 256, F)
for _k in range(8):
    SCRATCH["p%d" % _k] = ("psum", [128, 512], F)
SCRATCH["p1"] = ("psum", [128, 8, 64], F)
NDS = 64
SEMAPHORES = ["sv", "ss", "sp", "sgq"] + ["d%d" % k for k in range(NDS)] + [x + str(k) for x in ("rn", "rl") for k in range(6)]

A = AluOpType
ACT = ActivationFunctionType
UN = 2.0 ** -20
M1, MASK, M2 = 266305.0, 0x42108, 4369 * 2.0 ** -15
R256, R512 = 2.0 ** 11, 1.5 * 2.0 ** 12

CY, PCY, GA, LAT, XLAT, PLAT = 0.95, 0.5, 1.9, 240.0, 170.0, 100.0
DL, DR, DA, DF, RN, RL = 1800.0, 300.0, 2000.0, 4000.0, 4000.0, 2000.0
SG = ['f'] * 8
CM = 'ssssssff'
CO = ['ssssssss'] * 8
OM = ['ssss'] * 8
FOLD = '22222111'
SIDE = 'sssssv'
SPLIT = 'fsnrj'
CQ, UQ = 2, 128
SQ = [[32, 32], [32, 16, 16]]
BANKA = ['56'] * 6 + ['50', '52']
BANKS = ['6'] * 6 + ['63', '64']
BANKL = '55555555'
BANKO = ['77'] * 6 + ['70', '22']
URG = {'k': 0, 'c': 10, 'a': 10, 'o': 10, 'u': 15, 'y': 10}
STAG = 4.0
HOLD = {'v': 0.17, 's': 0.71, 'p': 0.51, 'g': 0.62, 'y': 0.58, 'r': 0.0}
PASSES, AHEAD = 6, 1000.0
PLAN = {}


def rank_program(g, core, T, topo):
    rank = T.rank_of(core)
    if rank is None:
        return
    nxt = T.cores[(rank + 1) % len(T.cores)]
    rid, pid = topo.addr(nxt, core)
    mask = topo.mask(core, nxt)
    neng = len(topo.engines(core, nxt))
    Q = {"v": g.vector, "s": g.scalar, "p": g.tensor, "g": g, "y": g.sync}
    ops = []
    wr, rd, ep = {}, {}, {}
    nd = [0]
    tag = ["k"]

    def cells(c, p):
        return np.concatenate([2 * c, 2 * c + 1]) if p is None else 2 * c + p

    def R(name, a=0, b=None, st=1, p=None):
        if b is None:
            b = SCRATCH[name][1][1]
        rows = slice(0, 128) if p is None else slice(64 * p, 64 * p + 64)
        c = np.arange(a, b, abs(st))
        cs = slice(a, b, st) if st > 1 else slice(a, b) if st > 0 else slice(b - 1, a - 1 if a > 0 else None, -1)
        return (T[name][rows, cs], name, cells(c, p), len(c))

    def R3(name, g0, a, b, st=1, ng=4):
        sh = SCRATCH[name][1][1:]
        c = np.arange(sh[0] * sh[1]).reshape(sh)[g0:g0 + ng, a:b:st].ravel()
        return (T[name][:, g0:g0 + ng, a:b:st], name, cells(c, None), len(c))

    def parts(step):
        return ((0, 2), (2, 2)) if step in SPLIT else ((0, 4),)

    def G(win, off):
        return (win[0].indirect(off[0]), win[1], win[2], win[3], off)

    def add(eng, fn, reads, writes, cost, lat=0.0, sem=None):
        me = len(ops); deps = set(); order = set()
        rs = []
        for r in reads:
            if isinstance(r, tuple):
                rs.append(r)
                if len(r) == 5:
                    rs.append(r[4])
        for r in rs + writes:
            nme = r[1]
            if nme not in wr:
                wr[nme] = np.full(2 * int(np.prod(SCRATCH[nme][1][1:])), -1); rd[nme] = []
            if SCRATCH[nme][0] == "psum":
                e = ep.setdefault(nme, [eng, [], []])
                if e[0] != eng:
                    ep[nme] = e = [eng, [], e[1]]
                deps.update(e[2])
                if eng == "p":
                    order.update(e[1])
                if me not in e[1]:
                    e[1].append(me)
        for r in rs:
            deps.update(int(x) for x in np.unique(wr[r[1]][r[2]]) if x >= 0)
        for w in writes:
            for x in np.unique(wr[w[1]][w[2]]):
                if x >= 0 and not (eng == "p" and ops[int(x)]["e"] == "p"):
                    deps.add(int(x))
            m = np.zeros(len(wr[w[1]]), bool); m[w[2]] = True
            keep = []
            for o, c in rd[w[1]]:
                if m[c].any():
                    deps.add(o)
                    c = c[~m[c]]
                if len(c):
                    keep.append((o, c))
            rd[w[1]] = keep
        for r in rs:
            rd[r[1]].append((me, r[2]))
        for w in writes:
            wr[w[1]][w[2]] = me
        deps.discard(me); order.discard(me)
        ops.append({"e": eng, "f": fn, "d": deps, "o": order, "c": cost, "l": lat, "sem": sem, "t": tag[0]})
        return me

    def ap(x):
        return x[0] if isinstance(x, tuple) else x

    def ps(x):
        return SCRATCH[x[1]][0] == "psum"

    def vc(o, i, k=1.0):
        return 50 + o[3] * GA * CY if len(i) == 5 else max(64, o[3] * k) * CY

    def half(*x):
        return 0.5 if all(SCRATCH[y[1]][2] in (B, U) for y in x) else 1.0

    def tt(o, a, b, op):
        return add("v", lambda: g.vector.tensor_tensor(o[0], a[0], b[0], op), [a, b], [o], vc(o, a, 1.0 if ps(a) or ps(b) else 2.0))

    def ts(o, a, s1, op0, s2=None, op1=None):
        if op1 is None:
            return add("v", lambda: g.vector.tensor_scalar(o[0], a[0], ap(s1), None, op0), [a, s1], [o], vc(o, a, half(o, a)))
        return add("v", lambda: g.vector.tensor_scalar(o[0], a[0], ap(s1), ap(s2), op0, op1), [a, s1, s2], [o], vc(o, a, half(o, a)))

    def cp(o, a):
        return add("v", lambda: g.vector.tensor_copy(o[0], a[0]), [a], [o], vc(o, a, half(o, a)))

    def ms(o, c):
        return add("v", lambda: g.vector.memset(o[0], c), [], [o], vc(o, o, half(o)))

    def scan(o, a, b, init, op0, op1):
        return add("v", lambda: g.vector.tensor_tensor_scan(o[0], a[0], b[0], init, op0, op1), [a, b], [o], vc(o, a, half(o, a, b)))

    def act(o, a, scale=1.0, bias=0.0, fn=ACT.Copy):
        if isinstance(scale, tuple):
            return add("s", lambda: g.scalar.activation(o[0], a[0], fn, scale=scale[0]), [a, scale], [o], vc(o, a) + 15)
        if bias == 0.0 and scale == 1.0:
            return add("s", lambda: g.scalar.activation(o[0], a[0], fn), [a], [o], vc(o, a) + 15)
        return add("s", lambda: g.scalar.activation(o[0], a[0], fn, bias=bias, scale=scale), [a], [o], vc(o, a) + 15)

    def un(eng, o, a, scale, bias):
        if eng == "v":
            ts(o, a, scale, A.mult, bias, A.add)
        else:
            act(o, a, scale, bias)

    def gather(eng, o, w):
        if eng == "v":
            cp(o, w)
        else:
            act(o, w)

    def mm(lst):
        def fn():
            r = None
            for o, l, x, a, b in lst:
                r = g.tensor.matmul(o[0], l[0], x[0], a, b)
            return r
        c = sum(max(64, x[3]) * (4 if SCRATCH[x[1]][2] == F else 1) for o, l, x, a, b in lst) * PCY
        return add("p", fn, [q[1] for q in lst] + [q[2] for q in lst], [q[0] for q in lst], c, PLAT)

    def grp(o, terms):
        return [(o, l, x, k == 0, k == len(terms) - 1) for k, (l, x) in enumerate(terms)]

    def iota(o, pat, base, cm):
        if SCRATCH[o[1]][2] == I:
            fn = lambda: g.iota(o[0], pat, base, cm)
        else:
            fn = lambda: g.iota(o[0], pat, base, cm, allow_small_or_imprecise_dtypes=True)
        return add("g", fn, [], [o], 130 + 2 * o[3] * CY)

    def asel(o, a, pat, base):
        return add("g", lambda: g.affine_select(o[0], a[0], pat, A.is_equal, 0.0, base, -1), [a], [o], 170 + 2 * o[3] * CY)

    def newsem():
        nd[0] += 1
        return "d%d" % (nd[0] - 1)

    def dma(eng, o, i, reads, writes, nbytes, more=0.0, **kw):
        s = newsem()
        return add(eng, lambda: Q[eng].dma_start(o, i, **kw).then_inc(T.sem[s], 16), reads, writes,
                   900.0 if eng == "g" else 60.0, DL + more + nbytes / DR, (s, 16))

    def send(src, dst, rs, wait):
        s = newsem()
        a = add("g", lambda: g.remote_dma(dst[0], src[0], T.sem[rs], T.sem[s], pid, rid, mask), [src], [], 300.0, 1000.0, (s, neng))
        b = add("r", None, [], [dst], 0.0, wait, (rs, neng))
        ops[b]["o"].add(a)

    dma("y", R("fpi")[0], T.fp[:], [], [R("fpi")], 4096)
    dma("s", R("pxi")[0], T.px[:], [], [R("pxi")], 294912)
    dma("y", R("lsi")[0], T.ls[:], [], [R("lsi")], 65536)
    dma("y", R("tsg", 0, 2304)[0], T.sg[:], [], [R("tsg", 0, 2304)], 589824, 1500.0)
    dma("s", R("omi")[0], T.om[:], [], [R("omi")], 16384)
    dma("y", R("tco", 0, 2304)[0], T.co[:], [], [R("tco", 0, 2304)], 589824, 4000.0)

    def C(k):
        return R("col", k, k + 1)

    def P(k):
        return R("pid", k, k + 1)
    ms(R("ones"), 1.0); ms(R("hl", 0, 64), UN)
    asel(R("pls", p=0), R("hl", 0, 64, p=0), [[1, 16], [16, 4]], 0)
    asel(R("ppx", p=0), R("hl", 0, 64, p=0), [[-1, 16], [16, 4]], 15)
    act(R("pls", p=1), R("pls", p=0)); act(R("ppx", p=1), R("ppx", p=0))
    asel(R("id32"), R("ones"), [[1, 128]], 0)
    iota(R("pid", 0, 1), [[0, 1]], 0, 1)
    iota(R("q8"), [[-16, 8]], 0, 1)
    iota(R("oci", 0, 4), [[1, 4]], 0, 0)
    iota(R("oci", 4, 14), [[1, 10]], 3, 0)
    iota(R("oci", 16, 18), [[64, 2]], 0, 0)
    iota(R("dgi"), [[0, 9], [-1, 16]], 16, 1)
    iota(R("tq", 0, 192), [[0, 4], [1, 48]], -64, 0)
    for q in range(4):
        iota(R("yy", 16 * q, 16 * q + 16), [[4, 2], [8, 2], [0, 4]], 1 + (q >> 1) + 2 * (q & 1), 0)
    act(R("idb"), R("id32")); act(R("idm"), R("id32"), -16.0 / UN)
    ts(P(1), P(0), 15, A.bitwise_and)
    ts(C(2), P(1), 0.0, A.is_equal)
    ts(C(5), C(2), -1048576.0, A.mult, 2176.0, A.add)
    ts(C(6), C(2), -1048576.0, A.mult, -1024.0, A.add)
    ts(C(7), C(2), 2304.0, A.mult)
    ms(R("tsg", 2304, WT), 16.0); ms(R("tco", 2304, WT), 0.0)
    ts(R("q8"), R("q8"), 4, A.arith_shift_right)
    ts(R("blk"), R("q8"), 0.0, A.is_equal)
    ts(R("n8", 0, 4), R("q8", 0, 4), 3, A.bitwise_and)
    ts(R("bl4", 0, 4), R("n8", 0, 4), 0.0, A.is_equal)
    ms(R("bl4", 4, 8), 0.0)
    for k, x in enumerate((2048.0, -1.0, 0.0, 2.0, 2.0 ** 30, 0.0, 2048.0, 1.0)):
        act(R("rh", 8 * k, 8 * k + 8), R("blk"), x)
    ts(R("dgi"), R("dgi"), 15, A.bitwise_and)
    ts(R("dg"), R("dgi"), 0.0, A.is_equal)
    ms(R("dg", 0, 16, p=0), 0.0); ms(R("dg", 80, 144, p=0), 0.0); ms(R("dg", 16, 80, p=1), 0.0)
    ts(R("oci", 4, 14), R("oci", 4, 14), 3, A.bitwise_and)
    ts(P(2), P(0), 12, A.bitwise_and); ts(P(3), P(0), 3, A.bitwise_and); ts(P(4), P(0), 2, A.arith_shift_right, 12, A.bitwise_and)
    ts(C(8), P(2), 4.0, A.mult); tt(C(9), P(3), P(4), A.add)
    ts(R("oci", 16, 18), R("oci", 16, 18), C(8), A.add, C(9), A.add)
    cp(R("oc", 0, 14), R("oci", 0, 14)); cp(R("oc", 16, 18), R("oci", 16, 18))
    ms(R("rst"), 1.0); ms(R("rr", 0, 272, 136), 1.0); ms(R("ff", 0, 272, 136), 500 * UN)
    act(R("idh"), R("id32"), 0.5); act(R("nidh"), R("id32"), -0.5); act(R("idz"), R("id32"), -0.5)
    act(R("idl"), R("id32"), -4096.0);
    act(R("c1"), R("ones", 0, 64)); act(R("c100"), R("ones"), -100 * UN)
    mid = 44 if SIDE[1] == "s" else 144
    act(R("c44"), R("ones"), mid * UN); act(R("c44", 0, 128, 32), R("ones", 0, 4), (mid + 300) * UN)
    ms(R("ct"), 4096.0); ms(R("ct", 0, 128, 16), 8192.0)
    act(R("posc"), R("yy", 0, 64), 1.0, 144 * UN)
    act(R3("p1", 4, 0, 48), R("tq", 0, 192), M1)
    ms(R("rstm"), -2.0 ** 30); ms(R("rstm", 0, 192, 48), 64 * M1)
    tag[0] = "fa0"
    act(R("nidb"), R("id32"), -1.0)
    for x in ("cc0", "cc1", "ca0", "ca1", "cb0", "cb1"):
        cp(R(x, 2048, 4128, 2064), R("bl4", 4, 6))
    cp(R("idf"), R("id32")); ts(R("nidf"), R("id32"), -1.0, A.mult)
    tag[0] = "fk0"
    iota(R("sel"), [[0, 2048]], 1, 0)
    asel(R("sel"), R("sel"), [[1, 16], [16, 8], [0, 16]], 0)

    def turn(o, oc, src, sc, mat):
        return [(R(o, oc, oc + 64, p=p), R(src, sc, sc + 64, p=p), R(mat, 0, 64, p=p) if SCRATCH[mat][1][1] == 64
                 else R(mat, 64 * p, 64 * p + 64, p=p), True, True) for p in range(2)]

    def records(dst, src, c):
        ts(R("ea", c, c + 64), R(src, c, c + 64), 0xFFF00, A.bitwise_and)
        ts(R("ec", c, c + 64), R("ea", c, c + 64), 2.0, A.mult, 400.0, A.add)
        tt(R(dst, c, c + 64), R("ec", c, c + 64), R(src, c, c + 64), A.subtract)

    def listkeys(u, dst, c):
        ts(R("hl", c, c + 64), R(u, 0, 64), R256 - 128 * UN, A.add, R256, A.subtract)
        tt(R(u, 0, 60), R(u, 0, 60), R("hl", c + 4, c + 64), A.min)
        tt(R(dst, c, c + 64), R(u, 0, 64), R("hl", c, c + 64), A.add)

    def tables():
        ts(R("tn"), R("pxi"), 257.0, A.add)
        act(R("pxh"), R("tn"), 1.0, 2.0 ** 31 - 128)
        act(R("pxh"), R("pxh"), 1.0, -2.0 ** 31)
        for k in range(2):
            a = 288 * k
            mm(grp(R("p%d" % (5 + k), 0, 288), [(R("idz"), R("tn", a, a + 288)), (R("id32"), R("pxh", a, a + 288))]))
            act(R("tn", a, a + 288), R("p%d" % (5 + k), 0, 288), 2.0, 145.0)

    def bounds():
        cp(R("omf"), R("omi"))
        for k in range(4):
            act(R("omx", k, 128, 4), R("omf"), R("bl4", k, k + 1))
        mm(grp(R("p7", 0, 128), [(R("dg", 16, 144), R("omx"))]))
        act(R("omy"), R("p7", 0, 128))
        act(R("nb"), G(R("omy"), R("oc", 16, 18)), -1.0, 1.0)

    def pixels(v, H):
        c, w = 64 * H, "p%d" % (3 + H)
        if v == 0:
            cp(R("n0", 8 * H, 8 * H + 4), R("fpi", 4 * H, 4 * H + 4))
            cp(R("pg", c, c + 64), G(R("pxi"), R("n0", 8 * H, 8 * H + 4)))
            records("pe", "pg", c)
        else:
            act(R("pe", c, c + 64), G(R("tn"), R("n%d" % v, 8 * H, 8 * H + 4)))
        mm(turn(w, 128, "pe", c, "ppx"))
        ts(R("hp", c, c + 64), R(w, 128, 192), R256 - 128 * UN, A.add, R256, A.subtract)
        un(SIDE[4] if v else "v", R("hb", c, c + 64), R("hp", c, c + 64), 1.0, -200 * UN)
        tt(R(w, 132, 192), R(w, 132, 192), R("hp", c, c + 60), A.min)
        tt(R(w, 128, 192), R(w, 128, 192), R("hb", c, c + 64), A.add)

    def front(v, H):
        b, u, w, c = str(v & 1), "p%d" % (2 * H), "p%d" % (3 + H), 128 * H
        last = v == NV - 1

        def L(nme, a=0, e=128, st=1, p=None):
            return R(nme, c + a, c + e, st, p)
        x, y = R(w, 128, 192), R("l%d" % v, 64 * H, 64 * H + 64)
        for o in ("ma", "mb", "ma"):
            tt(L(o, 0, 128, 2), x, y, A.min); tt(L(o, 1, 128, 2), x, y, A.max)
            x, y = L(o, 0, 64), L(o, 64, 128)
        for h, (o, oc) in enumerate(((u, 128), ("mc", 64 * H))):
            x, y = L("ma", 32 * h, 32 * h + 32), L("ma", 64 + 32 * h, 96 + 32 * h)
            tt(R(o, oc, oc + 64, 2), x, y, A.min); tt(R(o, oc + 1, oc + 64, 2), x, y, A.max)
        x, y = R(u, 128, 192), R("mc", 64 * H, 64 * H + 64)
        tt(R(u, 0, 128, 2), x, y, A.min); tt(R(u, 1, 128, 2), x, y, A.max)
        for g0, ng in parts("f"):
            a, z = 32 * g0, 32 * (g0 + ng)
            ts(L("hh", a, z), R(u, a, z), R512, A.add, R512, A.subtract)
            tt(L("xf", a, z), R(u, a, z), L("hh", a, z), A.subtract)
        un(SIDE[0], L("slb"), L("hh"), 8.0, 128 - 128.5 / 256)
        ts(L("yf"), L("xf"), -8.0, A.mult, -200 * UN, A.add)
        scan(L("bf"), L("yf"), L("xf"), -56 * UN, A.max, A.min)
        scan(L("af"), L("yf"), L("xf"), 144 * UN, A.min, A.max)
        for t, src, bank, oc, k in (("b", "bf", u, 256, -1024.0), ("a", "af", w, 0, 2176.0)):
            mm([(R(bank, oc + 64 * h, oc + 64 * h + 64, p=p), L(nme, h, 128, 2, p), R(idn, 64 * p, 64 * p + 64, p=p), st, not st)
                for h in range(2) for p in range(2) for nme, idn, st in (("slb", "idb", True), (src, "idm", False))])
            o = "o" + t + b
            ts(L(o, 0, 64), R(bank, oc, oc + 64), C(5 + (t == "b")), A.add, C(7), A.max)
            ts(L(o, 64, 128), R(bank, oc + 64, oc + 128), k, A.add)
        scan(L("ln", 0, 127), L("hh", 1, 128), L("hh", 0, 127), 0.0, A.max, A.subtract)
        ts(L("ln", 31, 128, 32), L("hh", 31, 128, 32), -1.0, A.mult, 4097 * 512 * UN, A.add)
        ss, e = "ss" + b, 2048 * H
        how = SG[2 * v + H]
        fused = how == "f"
        k = 0
        for h in range(2):
            a = 0
            for n in SQ[h]:
                o = (e + 32 * a + h, e + 32 * (a + n), 2)
                wa, wb = (G(R("tsg"), L(x + b, 64 * h + a, 64 * h + a + n)) for x in ("oa", "ob"))
                if fused:
                    act(R("sb", *o), wb); tt(R(ss, *o), wa, R("sb", *o), A.add)
                else:
                    gather(how[k % len(how)], R("sb", *o), wb); gather(how[(k + 1) % len(how)], R(ss, *o), wa)
                a += n; k += 2
            for s0 in (h, 16 + h):
                lst = []
                for s in range(s0, s0 + 16, 2):
                    lst += grp(R(w, s, 512, 32, 0), [(R(ss, e + s, e + 2048, 32), R("rh", 0, 16) if s else R("rh", 16, 32))]
                               + ([] if last and fused or s == 0 else [(R("sb", e + s, e + 2048, 32), R("rh", 16, 32) if fused else R("rh", 48, 64))])
                               + ([(R("c1", 0, 64), R("rh", 32, 48))] if s == 31 else []))
                mm(lst)
        if not fused:
            tag[0] = "fa" + tag[0][2]
            x, y = R(ss, e, e + 2048), R("sb", e, e + 2048)
            dma("g", x[0], y[0], [x, y], [x], 1 << 19, DA, accum_op=A.add)
        tag[0] = "ww" + tag[0][2]
        if not last:
            act(L("ln", 0, 128, 32), R("ones", 0, 4))
        act(R(u, 0, 128), L("ln"), -0.5, 1.0)
        act(L("rst", 0, 128, 32), R("nb", 8 * v + 4 * H, 8 * v + 4 * H + 4))
        if not last:
            act(L("den"), L("ln"), -2048.0, 1.0, ACT.Relu)
            act(L("zc"), L("hh"), -0.5, 1.0)
            mm(grp(R(u, 256, 384), [(R("idb"), R("c100")), (R("idh"), L("af")), (R("nidh"), L("bf"))])
               + grp(R(u, 384, 512), [(R("idb"), R("c44")), (R("idb"), L("den"))]
                     + ([(R("nidh"), L("af")), (R("nidh"), L("bf"))] if SIDE[1] == "s" else [(R("nidb"), L("af"))])))

    def seen(v, H):
        u, w, c, d = "p%d" % (2 * H), "p%d" % (3 + H), 128 * H, 136 * H
        for p in range(2):
            tt(R("nw", c, c + 128, p=p), R(w, 128 * p, 128 * p + 128, p=0), R("ln", c, c + 128, p=p), A.mult)
        if v < NV - 1:
            for p in range(2):
                if SIDE[1] == "s":
                    act(R("tc", c, c + 128, p=p), R(w, 256 + 128 * p, 384 + 128 * p, p=0), 1.0, -0.5, ACT.Sign)
                else:
                    ts(R("tc", c, c + 128, p=p), R(w, 256 + 128 * p, 384 + 128 * p, p=0), 0.0, A.is_gt, 2.0, A.mult)
        for g0, ng in parts("s"):
            a, z = 32 * g0, 32 * (g0 + ng)
            scan(R("rr", d + a + 1, d + z + 1), R("nw", c + a, c + z), R("rst", c + a, c + z), 1.0, A.add, A.min)
            tt(R("lv", c + a, c + z), R(u, a, z), R("rr", d + a, d + z), A.max)

    def remake(v, H):
        u, w, c, d, e, k = "p%d" % (2 * H), "p%d" % (3 + H), 128 * H, 136 * H, 192 * H, 64 * H
        nm, un_ = "nm%d" % (v & 1), tag[0][1:]

        def L(nme, a=0, z=128, st=1):
            return R(nme, c + a, c + z, st)

        def S(nme):
            return R(nme, 4 * H, 4 * H + 4)

        def J(nme, a=0, st=1):
            return R(nme, e + a, e + 192, st)
        for g0, ng in parts("n"):
            a, z = 32 * g0, 32 * (g0 + ng)
            tt(L("nm", a, z), R(u, 256 + a, 256 + z), L("tc", a, z), A.mult)
            tt(R(u, a, z), R(u, 384 + a, 384 + z), L("nm", a, z), A.add)
            tt(R(u, 128 + a, 128 + z), R(u, a, z), L("zc", a, z), A.add)
            scan(L("zz", a, z, -1), R(u, 128 + a, 128 + z, -1), R("rr", d + a, d + z, -1), 1.0, A.min, A.max)
        tag[0] = "n" + un_
        ts(S("e8"), L("zz", 1, 128, 32), 4.0 / UN, A.mult)
        ts(S("n8"), S("e8"), 1023, A.bitwise_and)
        ts(S("q8"), S("e8"), 20, A.arith_shift_right)
        tt(R("nam", 8 * H, 8 * H + 4), S("n8"), S("q8"), A.subtract)
        tt(R("nx", 144 * H, 144 * H + 144), G(R("nam", 8 * H, 8 * H + 4), R("oc", 4, 13)), R("dg"), A.mult)
        mm([(R(w, 0, 8), R("nx", 144 * H + 16, 144 * H + 144), R("bl4"), True, True),
            (R(w, 8, 16), R("nx", 144 * H, 144 * H + 128), R("bl4"), True, True)])
        ts(R(nm, 16 * H, 16 * H + 16), R(w, 0, 16), 3.0, A.add)
        send(R(nm, 16 * H + 8, 16 * H + 12), R("n%d" % (v + 1), 8 * H, 8 * H + 4), "rn%d" % (2 * v + H), RN)
        un(SIDE[2], R("te", k, k + 64), G(R("tn"), R(nm, 16 * H, 16 * H + 4)), -UN, 1 + 144 * UN)
        mm(turn(w, 64, "te", k, "id32"))
        tt(R("t8", 8 * H, 8 * H + 4), S("e8"), S("n8"), A.subtract)
        un(SIDE[3], R("thb", k, k + 64), G(R("t8", 8 * H, 8 * H + 4), R("oc", 0, 4)), UN / 4, 0.0)
        tag[0] = "r" + un_
        for g0, ng in parts("r"):
            a, z = 32 * g0, 32 * (g0 + ng)
            scan(R("ff", d + a + 1, d + z + 1), L("ln", a, z), R(u, a, z), 500 * UN, A.max, A.min)
            tt(R(u, a, z), R(u, a, z), R("ff", d + a, d + z), A.not_equal)
            tt(R3("live", 4 * H + g0, 0, 32, 1, ng), R(u, a, z), L("lv", a, z), A.is_gt)
            tt(R3("p1", g0, 0, 32, 1, ng), R(u, 128 + a, 128 + z), R3("live", 4 * H + g0, 0, 32, 1, ng), A.min)
        tt(R3("live", 4 * H, 32, 48), R(w, 64, 128), R("thb", k, k + 64), A.is_lt)
        tt(R3("p1", 0, 32, 48), R(w, 64, 128), R3("live", 4 * H, 32, 48), A.min)
        for g0, ng in parts("j"):
            a, z = 48 * g0, 48 * (g0 + ng)
            n2m, tq, ei, e1, e2 = (R(x, e + a, e + z) for x in ("n2m", "tq", "ei", "e1", "e2"))
            un(SIDE[5], n2m, R3("live", 4 * H + g0, 0, 48, 1, ng), M1, -M1)
            tt(tq, R3("p1", 4 + g0, 0, 48, 1, ng), R3("live", 4 * H + g0, 0, 48, 1, ng), A.mult)
            scan(R(u, a, z), R("rstm", a, z), n2m, 0.0, A.max, A.add)
            tt(ei, R(u, a, z), tq, A.add)
            ts(e1, ei, MASK, A.bitwise_and)
            ts(e2, e1, M2, A.mult)
            ts(e1, e2, 15, A.bitwise_and)
        f = 96 * H
        tt(R(u, 0, 96), R3("p1", 0, 0, 48, 2), J("e1", 0, 2), A.add)
        tt(R("ta", f, f + 96), R3("p1", 0, 1, 48, 2), J("e1", 1, 2), A.add)
        a, o = 0, "ta"
        for st in range(3):
            a2, o2 = 96 - a, ("tb" if o == "ta" else "ta")
            for h in range(2):
                x, y = R(u, a + h, a + 96, 2), R(o, f + h, f + 96, 2)
                for j, op in enumerate((A.min, A.max)):
                    tt(R(u, a2 + 48 * j, a2 + 48 * j + 48) if h == 0 else R(o2, f + 48 * j, f + 48 * j + 48), x, y, op)
            a, o = a2, o2
        for j, op in enumerate((A.min, A.max)):
            tt(R("yy", e + 96 * j, e + 96 * j + 96), R(u, a, a + 96), R(o, f, f + 96), op)
        tt(R(u, 192, 256), J("yy", 0, 3), J("yy", 1, 3), A.max)
        tt(R(u, 192, 256), R(u, 192, 256), J("yy", 2, 3), A.max)
        tt(R(u, 0, 64), R("posc"), R(u, 192, 256), A.subtract)
        listkeys(u, "o%d" % (v & 1), k)
        send(R("o%d" % (v & 1), k, k + 64), R("l%d" % (v + 1), k, k + 64), "rl%d" % (2 * v + H), RL)

    def floats(v, H):
        b, n, c, e = str(v & 1), 2 * v + H, 128 * H, 2048 * H
        al, lh, z = "al" + b, "lh" + b, 2064 * H
        tag[0] = "fa%d" % n
        bank = "p" + BANKL[n]
        lst = []
        for h in range(2):
            o = 64 * h
            lst += [(R(bank, o, o + 64), R("ct", 128 * h, 128 * h + 128), R("idb", 0, 64), True, False)]
            lst += [(R(bank, o, o + 64, p=p), R("lv", c + h, c + 128, 2, p), R("idl", 64 * p, 64 * p + 64, p=p), False, True) for p in range(2)]
        mm(lst)
        act(R(lh, 2 * c, 2 * c + 128), R(bank, 0, 128))
        tt(R(lh, 2 * c + 128, 2 * c + 256), R(bank, 0, 128), R(lh, 2 * c, 2 * c + 128), A.subtract)
        tag[0] = "fc%d" % n
        m = 64 // CQ
        joint = CM[n] == "f"
        cols = [("cc" + b, "idf", "nidf")] if joint else [("ca" + b, "idb", "nidb"), ("cb" + b, "idb", "nidb")]
        for q in range(CQ):
            for h in range(2):
                a, x = 32 * m * q + h, 32 * m * (q + 1)
                wa, wb = (G(R("tco"), R(o + b, c + 64 * h + m * q, c + 64 * h + m * (q + 1))) for o in ("oa", "ob"))
                gather(CO[n][(2 * q + h) % 4], R("cb" + b, z + a, z + x, 2), wb)
                if joint:
                    tt(R("cc" + b, z + a, z + x, 2), wa, R("cb" + b, z + a, z + x, 2), A.add)
                else:
                    gather(CO[n][4 + (2 * q + h) % 4], R("ca" + b, z + a, z + x, 2), wa)
        tag[0] = "fa%d" % n
        nb = 8 if FOLD[n] == "3" else 4
        bs, nj = 2048 // nb, 32 // nb
        for q in range(4):
            bank = "p" + BANKA[n][q % len(BANKA[n])]
            part = [(i // nj, i % nj) for i in range(8 * q, 8 * q + 8)]
            lst = []
            for i, (k, j) in enumerate(part):
                h, r = k & 1, (nb * j + k) >> 1
                lst += grp(R(bank, 64 * i, 64 * i + 64), [(R("sel", 128 * r, 128 * r + 128), R(lh, 2 * c + 128 * x + 64 * h, 2 * c + 128 * x + 64 * h + 64))
                                                         for x in range(1 if j + k == 0 else 2)])
            mm(lst)
            for i, (k, j) in enumerate(part):
                tt(R(al, e + bs * k + j, e + bs * k + bs, nj), R(bank, 64 * i, 64 * i + 64), R("ss" + b, e + nb * j + k, e + 2048, 32), A.mult)
        tag[0] = "fo%d" % n
        for k in range(nb):
            un(OM[n][k % 4], R("om" + b, e + k, e + 2048, nb), R(al, e + bs * k, e + bs * k + bs), -2.0 ** -17, 1.0)
        tag[0] = "fu%d" % n
        for k in range(4):
            bank = "p" + BANKS[n][k % len(BANKS[n])]; a = z + 512 * k
            mm(grp(R(bank), [(R(p), R(x, a + 1, a + 513)) for x, p, q in cols] + [(R(q), R(x, a, a + 512)) for x, p, q in cols]))
            a = e + 512 * k
            for x in range(0, 512, UQ):
                scan(R("ub", a + x, a + x + UQ, -1), R(bank, x, x + UQ, -1), R("om" + b, a + x, a + x + UQ, -1), 0.0, A.add, A.mult)
        tag[0] = "fy%d" % n
        ns = 32
        pt, pc = "p" + BANKO[n][0], "p" + BANKO[n][1]
        for k in range(int(FOLD[n])):
            ns //= 2
            x, y = R(al, e, e + 64 * ns), R(al, e + 64 * ns, e + 128 * ns)
            dma("g", x[0], y[0], [x, y], [x], 32768 * ns, DF if v < NV - 1 else DA, accum_op=A.add)
        for s0 in range(0, ns, 4):
            mm([(R(pt, 64, 128), R("id32"), R(al, e + bs * (s // nj) + s % nj, e + bs * (s // nj) + bs, nj), s == 0, s == ns - 1)
                for s in range(s0, s0 + 4)])
        act(R("yo" + b, c + 64, c + 128), R(pt, 64, 128), 2.0 ** -14, -8.0)
        mm(grp(R(pc, 0, 64), [(R(p), R(x, z + 1, z + 2048, 32)) for x, p, q in cols] + [(R("id32"), R("ub", e + 1, e + 2048, 32))]))
        act(R("yo" + b, c, c + 64), R(pc, 0, 64))
        for y, a in ((T.yt, c + 64), (T.yc, c)):
            dma("y", y[:, 64 * n:64 * n + 64], R("yo" + b, a, a + 64)[0], [R("yo" + b, a, a + 64)], [], 32768)

    for H in range(2):
        tag[0] = "mm%d" % H
        records("eb", "lsi", 64 * H)
        mm(turn("p%d" % (2 * H), 0, "eb", 64 * H, "pls"))
        listkeys("p%d" % (2 * H), "l0", 64 * H)
        pixels(0, H)
    tag[0] = "ww0"
    bounds(); tables()
    for n in range(2 * NV):
        v, H = n >> 1, n & 1
        tag[0] = "mm%d" % n
        front(v, H)
        tag[0] = "ss%d" % n
        seen(v, H)
        if v < NV - 1:
            tag[0] = "rr%d" % n
            remake(v, H)
            tag[0] = "mm%d" % (n + 2)
            pixels(v + 1, H)
        floats(v, H)

    n = len(ops)
    before = [sorted(o["d"] | o["o"]) for o in ops]
    after = [[] for _ in range(n)]
    for i in range(n):
        for d in before[i]:
            after[d].append(i)

    lag = [{d: (ops[d]["l"] + XLAT if ops[d]["e"] != o["e"] or ops[d]["sem"] else ops[d]["l"] + LAT if d in o["d"] else 0.0)
            for d in o["d"] | o["o"]} for o in ops]

    def sched(key, back):
        pre, post = (after, before) if back else (before, after)
        left = [len(x) for x in pre]
        rdy = [ops[i]["l"] if back else 0.0 for i in range(n)]
        free = {e: 0.0 for e in "vspgyr"}
        cand = {e: [] for e in free}
        at = [0.0] * n
        for i in range(n):
            if left[i] == 0:
                cand[ops[i]["e"]].append(i)
        for step in range(n):
            best = None
            for e in cand:
                if cand[e]:
                    t = max(free[e], min(rdy[i] for i in cand[e]))
                    i = min((i for i in cand[e] if rdy[i] <= t), key=lambda j: key[j])
                    soon = [j for j in cand[e] if t < rdy[j] <= t + HOLD[e] * ops[i]["c"] and key[j] < key[i] - AHEAD]
                    if soon:
                        x = min(rdy[j] for j in soon)
                        fit = [j for j in cand[e] if rdy[j] <= t and ops[j]["c"] <= x - t + 40]
                        i = min(fit, key=lambda j: key[j]) if fit else min(soon, key=lambda j: rdy[j])
                    t = max(t, rdy[i])
                    if best is None or t < best[0]:
                        best = (t, e, i)
            t, e, i = best
            cand[e].remove(i); at[i] = t
            free[e] = t + ops[i]["c"]
            for j in post[i]:
                rdy[j] = max(rdy[j], free[e] + (lag[i][j] if back else lag[j][i]))
                left[j] -= 1
                if left[j] == 0:
                    cand[ops[j]["e"]].append(j)
        return at

    if "plan" not in PLAN:
        pr = [0.0] * n
        for i in range(n - 1, -1, -1):
            pr[i] = ops[i]["c"] + max([pr[j] + lag[j][i] for j in after[i]] + [ops[i]["l"]])
        key = [-pr[i] - (1000.0 * URG[o["t"][1]] if o["t"][0] == "f" else 0.0 if o["t"] == "k" or int(o["t"][2]) & 1 else 1000.0 * STAG)
               for i, o in enumerate(ops)]
        best = None
        for k in range(PASSES):
            at = sched(key, False)
            end = max(at[i] + ops[i]["c"] + ops[i]["l"] for i in range(n))
            if best is None or end < best[0]:
                best = (end, at)
            bt = sched([-at[i] - ops[i]["c"] for i in range(n)], True)
            key = [-bt[i] - ops[i]["c"] for i in range(n)]
        at = best[1]
        gl = sorted(range(n), key=lambda i: (at[i], i))
        PLAN["plan"] = (best[0], {e: [i for i in gl if ops[i]["e"] == e] for e in "vspgyr"}, gl, [at[i] + ops[i]["c"] + ops[i]["l"] for i in range(n)])
    PLAN["ops"] = ops
    seq, glob = PLAN["plan"][1:3]
    gpos = {i: k for k, i in enumerate(glob)}

    esem = {"v": "sv", "s": "ss", "p": "sp", "g": "sgq"}
    place = {}
    for e in seq:
        for k, i in enumerate(seq[e]):
            place[i] = k + 1
    know = {e: {} for e in seq}
    snap = {}
    waits = {}
    need = set()
    for i in glob:
        o = ops[i]; e = o["e"]; kn = know[e]; want = {}
        for d in o["d"]:
            key, val = (ops[d]["sem"][0], 1) if ops[d]["sem"] else (ops[d]["e"], place[d])
            if val > want.get(key, (0, 0))[0]:
                want[key] = (val, d)
        w = []
        for key, (val, d) in sorted(want.items(), key=lambda x: -gpos[x[1][1]]):
            if kn.get(key, 0) >= val:
                continue
            w.append(d); need.add(d); kn[key] = val
            for k2, v2 in snap[d].items():
                if v2 > kn.get(k2, 0):
                    kn[k2] = v2
        waits[i] = w
        snap[i] = dict(kn)
    cnt = {e: 0 for e in esem}
    val = {}
    for e in esem:
        for i in seq[e]:
            if i in need and not ops[i]["sem"]:
                cnt[e] += 1; val[i] = cnt[e]
    for i in glob:
        o = ops[i]; e = o["e"]
        if e == "r":
            continue
        for d in waits[i]:
            if ops[d]["sem"]:
                Q[e].wait_ge(T.sem[ops[d]["sem"][0]], ops[d]["sem"][1])
            else:
                Q[e].wait_ge(T.sem[esem[ops[d]["e"]]], val[d])
        r = o["f"]()
        if i in val:
            r.then_inc(T.sem[esem[e]], 1)
    for i in glob:
        if ops[i]["sem"] and i not in need:
            g.wait_ge(T.sem[ops[i]["sem"][0]], ops[i]["sem"][1])
